import numpy as np
import ml_dtypes


def mxq(x, axis, fmt="e4m3"):
    dtype, down = {"e4m3": (ml_dtypes.float8_e4m3fn, 7), "e5m2": (ml_dtypes.float8_e5m2, 14)}[fmt]
    v = np.moveaxis(np.asarray(x, np.float32).astype(ml_dtypes.bfloat16).astype(np.float64), axis, -1)
    blocks = v.reshape(v.shape[:-1] + (-1, 32))
    amax = np.abs(blocks).max(-1, keepdims=True)
    byte = np.maximum(np.where(amax > 0, np.frexp(amax)[1] - 1 + 127, 0) - down, 1)
    scale = np.exp2(byte - 127.0)
    codes = (blocks / scale).astype(np.float32).astype(dtype).astype(np.float64)
    return np.moveaxis((codes * scale).reshape(v.shape), -1, axis)


WIDE = False


def mx_kscale(k):
    if not WIDE:
        return np.ones(k)
    levels = np.array([10, -10, 5, -5, 0])
    if k % 512:
        return np.exp2(np.random.permutation(np.resize(levels, k // 32))).repeat(32)
    a = np.empty((k // 512, 16))
    for p in range(k // 512):
        a[p, :8] = np.random.permutation(np.resize(levels, 8))
        for g in range(8):
            far = levels[np.abs(levels - a[p, g]) >= 10]
            a[p, g + 8] = far[np.random.randint(len(far))]
    return np.exp2(a.ravel()).repeat(32)


def f64(x):
    return np.asarray(x).astype(np.float64)


def striped(idx):
    return np.tile(idx.reshape(-1, 16).T, (8, 1)).astype(np.uint16)


def unstriped(offs):
    return offs[:16].T.reshape(-1).astype(np.int64)


E2M1 = np.array([0.0, 0.5, 1.0, 1.5, 2.0, 3.0, 4.0, 6.0, -0.0, -0.5, -1.0, -1.5, -2.0, -3.0, -4.0, -6.0])


def pack_weight(w, fmt):
    k, n = w.shape
    w = f64(np.asarray(w, np.float32).astype(ml_dtypes.bfloat16)).reshape(k // 32, 32, n)
    amax = np.abs(w).max(1)
    if fmt == "e4m3":
        byte = np.frexp(amax)[1] - 1 + 127 - 7
    else:
        mant, ex = np.frexp(amax / 6.0)
        byte = np.where(mant > 0.5, ex, ex - 1) + 127
    byte = np.clip(np.where(amax > 0, byte, 1), 1, 254)
    scaled = (w * np.exp2(127.0 - byte)[:, None, :]).reshape(k, n).astype(np.float32)
    by_word = np.ascontiguousarray(scaled.reshape(k // 512, 128, 4, n).transpose(0, 1, 3, 2))
    if fmt == "e4m3":
        words = by_word.astype(ml_dtypes.float8_e4m3fn).view(np.uint8)
    else:
        c = by_word.astype(ml_dtypes.float4_e2m1fn).view(np.uint8) & 0xF
        words = (c[..., 0::2] | (c[..., 1::2] << 4)).reshape(k // 512, 128, 2 * n)
    return np.ascontiguousarray(words), np.ascontiguousarray(byte.astype(np.uint8).reshape(k // 512, 16, n))


def unpack_weight(words, scales, fmt):
    g, _, n = scales.shape
    words = np.ascontiguousarray(words).reshape(g, 128, n, -1)
    if fmt == "e4m3":
        vals = words.view(ml_dtypes.float8_e4m3fn).astype(np.float64)
    else:
        nib = np.empty((g, 128, n, 4), np.uint8)
        nib[..., 0::2] = words & 0xF
        nib[..., 1::2] = words >> 4
        vals = E2M1[nib]
    vals = vals * np.repeat(np.exp2(scales.astype(np.float64) - 127.0), 8, axis=1)[..., None]
    return vals.transpose(0, 1, 3, 2).reshape(g * 512, n)


def gelu(v):
    return 0.5 * v * (1.0 + np.tanh(np.sqrt(2.0 / np.pi) * (v + 0.044715 * v**3)))


K, H, T, S, T2, S2 = 1024, 1024, 2048, 512, 4096, 1024

def setup_inputs():
    n = np.random.standard_normal
    s = mx_kscale(K)[:, None]
    u = mx_kscale(H)[:, None]
    tab_words, tab_scales = pack_weight(n((K, T)) * s, "e4m3")
    wl = (n((K, H)) / np.sqrt(K) / s * u.T).astype(np.float32)
    ws_words, ws_scales = pack_weight(n((K, H)) / np.sqrt(K) / s * u.T, "e2m1")
    bd = (0.5 * n(H) * u[:, 0]).astype(np.float32)
    tab2_words, tab2_scales = pack_weight(n((H, T2)) / np.sqrt(H) / u, "e4m3")
    bc = (0.5 * n(S2)).astype(np.float32)
    offs = striped(np.random.permutation(T)[:S])
    offs2 = striped(np.random.permutation(T2)[:S2])
    return {"tab_words": tab_words, "tab_scales": tab_scales, "offs": offs,
            "wl": wl, "ws_words": ws_words, "ws_scales": ws_scales, "bd": bd,
            "tab2_words": tab2_words, "tab2_scales": tab2_scales, "offs2": offs2, "bc": bc}

def reference(tab_words, tab_scales, offs, wl, ws_words, ws_scales, bd,
              tab2_words, tab2_scales, offs2, bc):
    v = unpack_weight(tab_words, tab_scales, "e4m3")[:, unstriped(offs)]
    v2 = unpack_weight(tab2_words, tab2_scales, "e4m3")[:, unstriped(offs2)]
    ws = unpack_weight(ws_words, ws_scales, "e2m1")
    a = mxq(f64(wl), 0, "e4m3").T @ v
    b = ws.T @ v
    h = np.abs(a - b - f64(bd)[:, None])
    y = v2.T @ mxq(h, 0, "e4m3")
    return 1.0 / (1.0 + np.exp(-(y + f64(bc)[:, None])))

@@ -1,0 +1,240 @@
+from contextlib import ExitStack
+
+import concourse.mybir as mybir
+from concourse.masks import make_identity
+
+K, H, T, S, T2, S2 = 1024, 1024, 2048, 512, 4096, 1024
+FLOPS = 2 * (2 * K * H * S + H * S2 * S)
+
+F32 = mybir.dt.float32
+BF16 = mybir.dt.bfloat16
+I32 = mybir.dt.int32
+U32 = mybir.dt.uint32
+U16 = mybir.dt.uint16
+U8 = mybir.dt.uint8
+FP8X4 = mybir.dt.float8_e4m3fn_x4
+FP4X4 = mybir.dt.float4_e2m1fn_x4
+ACT = mybir.ActivationFunctionType
+ALU = mybir.AluOpType
+
+P = 128
+PACK = 4
+K_PASS = P * PACK
+PASSES = 2
+QUADS = 4
+V2_ROW = (4, 8)
+M_VEC = {(0, 0): 0, (0, 1): 64, (1, 0): 64, (1, 1): 64}
+GATHER = 512
+
+
+def tile_list_session_drift_novelty_kernel(
+    tc, tab_words, tab_scales, offs, wl, ws_words, ws_scales, bd, tab2_words, tab2_scales, offs2, bc, out
+):
+    nc = tc.nc
+    with ExitStack() as ctx:
+        keep = ctx.enter_context(tc.tile_pool(name="keep", bufs=1))
+        psum = ctx.enter_context(tc.psum_pool(name="psum", bufs=1))
+
+        def tile(shape, dtype, name, tag=""):
+            return keep.tile(shape, dtype, name=name, tag=tag, align_bytes=64)
+
+        idx = keep.tile([P, S // 16], U16, name="idx")
+        idx2 = keep.tile([P, S2 // 16], U16, name="idx2")
+        ws_sraw = tile([P, PASSES, H // 4], I32, "ws_sraw")
+        tab_s = tile([P, PASSES, T // 4], I32, "tab_s")
+        tab2_s = tile([P, T2 // 4], I32, "tab2_s")
+        tab_w = [tile([P, T], I32, "tab_w%d" % a) for a in range(PASSES)]
+        banks = [psum.tile([P, S], F32, name="bank%d" % b) for b in range(8)]
+
+        ident = tile([P, P], F32, "ident")
+        bc_rows = tile([P, P], F32, "bc_rows")
+        bd_col = tile([P, 2, PACK], F32, "bd_col")
+        bc_col = tile([P, S2 // P], F32, "bc_col")
+        warm = tile([P, 1], F32, "warm")
+        nc.vector.memset(ws_sraw[:], 0)
+        nc.vector.memset(tab_s[:], 0)
+        nc.gpsimd.memset(bc_rows[:], 0.0)
+        nc.gpsimd.memset(tab2_s[:], 0)
+        make_identity(nc, ident[:])
+        nc.scalar.activation(warm[:], ident[:, 0:1], ACT.Sigmoid)
+
+        def load_idx():
+            nc.sync.dma_start(idx[:], offs)
+
+        def load_idx2():
+            nc.sync.dma_start(idx2[:], offs2)
+
+        def load_bc():
+            nc.sync.dma_start(bc_rows[0 : S2 // P, :], bc.rearrange("(u m) -> u m", m=P))
+
+        def load_bd():
+            nc.sync.dma_start(bd_col[:], bd.rearrange("(g p t) -> p g t", g=2, t=PACK))
+
+        def load_ws():
+            nc.sync.dma_start(ws_raw[:], ws_words.rearrange("a p c -> p a c").bitcast(I32))
+
+        def load_scale_rows(dst, src, r):
+            nc.sync.dma_start(dst[r:P:32, :, :], src[:, r:16:4, :].rearrange("a q c -> q a c").bitcast(I32))
+
+        def load_tab2_scale_rows(a, r):
+            nc.sync.dma_start(tab2_s[V2_ROW[a] + r : P : 32, :], tab2_scales[a, r:16:4, :].bitcast(I32))
+
+        def load_words(dst, src):
+            nc.sync.dma_start(dst[:], src.rearrange("p t i -> p (t i)").bitcast(I32))
+
+        def load_wl(g, a):
+            nc.sync.dma_start(
+                wl_raw[g, a][:],
+                wl[a * K_PASS : (a + 1) * K_PASS, g * K_PASS : (g + 1) * K_PASS].rearrange("(p j) c -> p j c", j=PACK),
+            )
+
+        ws_c = tile([P, PASSES * H * 2], U8, "ws_c")
+        ws_s = tile([P, PASSES * H], U8, "ws_s")
+        with tc.tile_pool(name="first", bufs=1) as first:
+            ws_raw = first.tile([P, PASSES, H // 2], I32, name="ws_raw")
+            load_ws()
+            load_idx()
+            load_bc()
+            load_bd()
+            load_idx2()
+            load_words(tab_w[0], tab_words[0])
+            load_scale_rows(ws_sraw, ws_scales, 0)
+            load_scale_rows(ws_sraw, ws_scales, 1)
+            load_scale_rows(ws_sraw, ws_scales, 2)
+            load_scale_rows(ws_sraw, ws_scales, 3)
+            load_scale_rows(tab_s, tab_scales, 0)
+            load_scale_rows(tab_s, tab_scales, 1)
+            load_words(tab_w[1], tab_words[1])
+            load_scale_rows(tab_s, tab_scales, 2)
+            load_scale_rows(tab_s, tab_scales, 3)
+            nc.vector.tensor_copy(
+                ws_c[:].bitcast(U16).rearrange("p (b t m) -> p b t m", t=PACK, m=P),
+                ws_raw[:].rearrange("p a c -> p (a c)").bitcast(U16).rearrange("p (b m t) -> p b t m", t=PACK, m=P),
+            )
+        late = ctx.enter_context(tc.tile_pool(name="late", bufs=1))
+        tab2_w = [late.tile([P, T2], I32, name="tab2_w%d" % a) for a in range(PASSES)]
+        wl_raw = {
+            (g, a): late.tile([P, PACK, K_PASS], F32, name="wl_raw%d%d" % (g, a), tag="wl_raw%d%d" % (g, a), align_bytes=64)
+            for g in range(2)
+            for a in range(PASSES)
+        }
+        load_wl(0, 0)
+        load_tab2_scale_rows(0, 0)
+        load_tab2_scale_rows(1, 0)
+        load_tab2_scale_rows(0, 1)
+        load_tab2_scale_rows(1, 1)
+        load_wl(0, 1)
+        load_tab2_scale_rows(0, 2)
+        load_tab2_scale_rows(1, 2)
+        load_tab2_scale_rows(0, 3)
+        load_tab2_scale_rows(1, 3)
+        load_wl(1, 0)
+        load_wl(1, 1)
+        load_words(tab2_w[0], tab2_words[0])
+        load_words(tab2_w[1], tab2_words[1])
+        nc.tensor.transpose(banks[7][:, 0:P], bc_rows[:], ident[:])
+        nc.scalar.activation(bc_col[:], banks[7][:, 0 : S2 // P], ACT.Copy)
+        nc.vector.tensor_copy(
+            ws_s[:].rearrange("p (b t m) -> p b t m", t=PACK, m=P),
+            ws_sraw[:].rearrange("p a c -> p (a c)").bitcast(U8).rearrange("p (b m t) -> p b t m", t=PACK, m=P),
+        )
+
+        v_c = [tile([P, S], U32, "v_c%d" % a) for a in range(PASSES)]
+        v_s = [tile([P, S], U8, "v_s%d" % a) for a in range(PASSES)]
+        for a in range(PASSES):
+            nc.vector.tensor_copy(v_c[a][:], tab_w[a][:].bitcast(U32).indirect(idx[:]))
+            nc.vector.tensor_copy(v_s[a][:], tab_s[:, a, :].bitcast(U8).indirect(idx[:]))
+
+        def short_term(g):
+            for a in range(PASSES):
+                for t in range(PACK):
+                    col = ((a * 2 + g) * PACK + t) * P
+                    nc.tensor.matmul_mx(
+                        out=banks[g * PACK + t][:],
+                        lhsT=ws_c[:, 2 * col : 2 * col + 2 * P].bitcast(FP4X4),
+                        lhsT_scale=ws_s[:, col : col + P],
+                        rhs=v_c[a][:].bitcast(FP8X4),
+                        rhs_scale=v_s[a][:],
+                        start=(a == 0),
+                        stop=False,
+                    )
+
+        v2_c = []
+        h_c = [tile([P, S], U32, "h_c%d" % g) for g in range(2)]
+        h_s = [tile([P, S], U8, "h_s%d" % g) for g in range(2)]
+
+        def quantise_wl(g, a):
+            raw = wl_raw[g, a]
+            neg = tile([P, PACK, P, PACK], BF16, "neg%d%d" % (g, a), "neg%d%d" % (g, a))
+            codes = tile([P, K_PASS], U32, "wl_c%d%d" % (g, a))
+            scales = tile([P, K_PASS], U8, "wl_s%d%d" % (g, a))
+            src = raw[:].rearrange("p j (m t) -> p m t j", t=PACK)
+            dst = neg[:].rearrange("p t m j -> p m t j")
+            cut = M_VEC[g, a]
+            nc.scalar.activation(dst[:, cut:P], src[:, cut:P], ACT.Copy, scale=-1.0)
+            if cut:
+                nc.vector.tensor_scalar(dst[:, 0:cut], src[:, 0:cut], -1.0, None, ALU.mult)
+            nc.vector.quantize_mx(
+                out=codes[:].bitcast(FP8X4), scales=scales[:], in_=neg[:].rearrange("p t m j -> p (t m j)")
+            )
+            for t in range(PACK):
+                nc.tensor.matmul_mx(
+                    out=banks[g * PACK + t][:],
+                    lhsT=codes[:, t * P : (t + 1) * P].bitcast(FP8X4),
+                    lhsT_scale=scales[:, t * P : (t + 1) * P],
+                    rhs=v_c[a][:].bitcast(FP8X4),
+                    rhs_scale=v_s[a][:],
+                    start=False,
+                    stop=(a == PASSES - 1),
+                )
+
+        def drift(g):
+            planes = late.tile([P, PACK, S], BF16, name="planes%d" % g, tag=("wl_raw10", "planes1")[g], align_bytes=64)
+            packed = tile([P, S, PACK], BF16, "packed%d" % g, "packed%d" % g)
+            for t in range(PACK):
+                nc.scalar.activation(planes[:, t, :], banks[g * PACK + t][:], ACT.Abs, bias=bd_col[:, g, t : t + 1])
+            nc.vector.tensor_copy(packed[:], planes[:].rearrange("p t n -> p n t"))
+            nc.vector.quantize_mx(
+                out=h_c[g][:].bitcast(FP8X4), scales=h_s[g][:], in_=packed[:].rearrange("p n t -> p (n t)")
+            )
+
+        def gather_v2(a, c):
+            nc.vector.tensor_copy(
+                v2_c[a][:, c * GATHER : (c + 1) * GATHER],
+                tab2_w[a][:].bitcast(U32).indirect(idx2[:, c * GATHER // 16 : (c + 1) * GATHER // 16]),
+            )
+
+        def score_pass(a, u):
+            nc.tensor.matmul_mx(
+                out=banks[u][:],
+                lhsT=v2_c[a][:, u * P : (u + 1) * P].bitcast(FP8X4),
+                lhsT_scale=v2_s[V2_ROW[a] : P, u * P : (u + 1) * P],
+                rhs=h_c[a][:].bitcast(FP8X4),
+                rhs_scale=h_s[a][:],
+                start=(a == 0),
+                stop=(a == PASSES - 1),
+            )
+
+        short_term(0)
+        quantise_wl(0, 0)
+        quantise_wl(0, 1)
+        v2_s = tile([P, S2], U8, "v2_s", "neg01")
+        nc.vector.tensor_copy(v2_s[:], tab2_s[:].bitcast(U8).indirect(idx2[:]))
+        short_term(1)
+        quantise_wl(1, 0)
+        quantise_wl(1, 1)
+        drift(0)
+        drift(1)
+        v2_c.append(tile([P, S2], U32, "v2_c0", "packed0"))
+        for c in range(S2 // GATHER):
+            gather_v2(0, c)
+        for u in range(S2 // P):
+            score_pass(0, u)
+        v2_c.append(tile([P, S2], U32, "v2_c1", "packed1"))
+        for c in range(S2 // GATHER):
+            gather_v2(1, c)
+        for u in range(S2 // P):
+            score_pass(1, u)
+            res = tile([P, S], F32, "res%d" % u)
+            nc.scalar.activation(res[:], banks[u][:], ACT.Sigmoid, bias=bc_col[:, u : u + 1])
+            nc.sync.dma_start(out[u * P : (u + 1) * P, :], res[:])

@@ -22,8 +22,8 @@ PACK = 4
 K_PASS = P * PACK
 PASSES = 2
 QUADS = 4
-V2_ROW = (4, 8)
-M_VEC = {(0, 0): 0, (0, 1): 64, (1, 0): 64, (1, 1): 64}
+V2_ROW = 4
+M_VEC = {(0, 0): 0, (0, 1): 64, (1, 0): 64, (1, 1): 128}
 GATHER = 512
 
 
@@ -41,22 +41,26 @@ def tile_list_session_drift_novelty_kernel(
         idx = keep.tile([P, S // 16], U16, name="idx")
         idx2 = keep.tile([P, S2 // 16], U16, name="idx2")
         ws_sraw = tile([P, PASSES, H // 4], I32, "ws_sraw")
-        tab_s = tile([P, PASSES, T // 4], I32, "tab_s")
-        tab2_s = tile([P, T2 // 4], I32, "tab2_s")
-        tab_w = [tile([P, T], I32, "tab_w%d" % a) for a in range(PASSES)]
+        ws_raw = tile([P, PASSES, H // 2], I32, "ws_raw")
+        v_s = tile([P, PASSES, S // 4], I32, "v_s")
+        v2_s = tile([P, PASSES, S2 // 4], I32, "v2_s")
+        v_g = tile([P, S], U8, "v_g")
+        v2_g = tile([P, S2], U8, "v2_g", "v2_g")
+        tab2_s = tile([P, T2 // 4], I32, "tab2_s", "tab2_s")
         banks = [psum.tile([P, S], F32, name="bank%d" % b) for b in range(8)]
 
         ident = tile([P, P], F32, "ident")
-        bc_rows = tile([P, P], F32, "bc_rows")
         bd_col = tile([P, 2, PACK], F32, "bd_col")
         bc_col = tile([P, S2 // P], F32, "bc_col")
-        warm = tile([P, 1], F32, "warm")
-        nc.vector.memset(ws_sraw[:], 0)
-        nc.vector.memset(tab_s[:], 0)
-        nc.gpsimd.memset(bc_rows[:], 0.0)
-        nc.gpsimd.memset(tab2_s[:], 0)
-        make_identity(nc, ident[:])
-        nc.scalar.activation(warm[:], ident[:, 0:1], ACT.Sigmoid)
+        with tc.tile_pool(name="warm", bufs=1) as warm_pool:
+            warm_in = warm_pool.tile([P, 8], F32, name="warm_in")
+            warm = warm_pool.tile([P, 8], F32, name="warm")
+            nc.gpsimd.memset(warm_in[:], 0.0)
+            nc.scalar.activation(warm[:], warm_in[:], ACT.Sigmoid)
+        mid = ctx.enter_context(tc.tile_pool(name="mid", bufs=1))
+        tab_w = [tile([P, T], I32, "tab_w0"), mid.tile([P, T], I32, name="tab_w1")]
+        bc_rows = tile([P, P], F32, "bc_rows")
+        wl_raw = {(0, 0): mid.tile([P, PACK, K_PASS], F32, name="wl_raw00")}
 
         def load_idx():
             nc.sync.dma_start(idx[:], offs)
@@ -76,8 +80,11 @@ def tile_list_session_drift_novelty_kernel(
         def load_scale_rows(dst, src, r):
             nc.sync.dma_start(dst[r:P:32, :, :], src[:, r:16:4, :].rearrange("a q c -> q a c").bitcast(I32))
 
-        def load_tab2_scale_rows(a, r):
-            nc.sync.dma_start(tab2_s[V2_ROW[a] + r : P : 32, :], tab2_scales[a, r:16:4, :].bitcast(I32))
+        def load_scale_table(dst, src):
+            nc.sync.dma_start(dst[0:P:4, :], src.rearrange("a q c -> q a c").bitcast(I32))
+
+        def move_scale_rows(dst, row, src, q):
+            nc.sync.dma_start(dst[32 * q + row : 32 * q + row + 4, :, :], src[32 * q : 32 * q + 32 : 4, :].bitcast(I32))
 
         def load_words(dst, src):
             nc.sync.dma_start(dst[:], src.rearrange("p t i -> p (t i)").bitcast(I32))
@@ -91,62 +98,58 @@ def tile_list_session_drift_novelty_kernel(
         ws_c = tile([P, PASSES * H * 2], U8, "ws_c")
         ws_s = tile([P, PASSES * H], U8, "ws_s")
         with tc.tile_pool(name="first", bufs=1) as first:
-            ws_raw = first.tile([P, PASSES, H // 2], I32, name="ws_raw")
+            tab_s = first.tile([P, T // 4], I32, name="tab_s")
+            nc.vector.memset(tab_s[:], 0)
+            nc.vector.memset(tab2_s[:], 0)
+            nc.gpsimd.memset(ws_sraw[:], 0)
+            nc.gpsimd.memset(v_s[:], 0)
+            make_identity(nc, ident[:])
+            nc.gpsimd.memset(v2_s[:], 0)
+            nc.gpsimd.memset(bc_rows[:], 0.0)
             load_ws()
             load_idx()
-            load_bc()
-            load_bd()
             load_idx2()
+            load_bd()
             load_words(tab_w[0], tab_words[0])
-            load_scale_rows(ws_sraw, ws_scales, 0)
-            load_scale_rows(ws_sraw, ws_scales, 1)
-            load_scale_rows(ws_sraw, ws_scales, 2)
-            load_scale_rows(ws_sraw, ws_scales, 3)
-            load_scale_rows(tab_s, tab_scales, 0)
-            load_scale_rows(tab_s, tab_scales, 1)
+            load_scale_table(tab_s, tab_scales)
+            for r in range(4):
+                load_scale_rows(ws_sraw, ws_scales, r)
+            load_scale_table(tab2_s, tab2_scales)
+            load_bc()
             load_words(tab_w[1], tab_words[1])
-            load_scale_rows(tab_s, tab_scales, 2)
-            load_scale_rows(tab_s, tab_scales, 3)
+            load_wl(0, 0)
             nc.vector.tensor_copy(
                 ws_c[:].bitcast(U16).rearrange("p (b t m) -> p b t m", t=PACK, m=P),
                 ws_raw[:].rearrange("p a c -> p (a c)").bitcast(U16).rearrange("p (b m t) -> p b t m", t=PACK, m=P),
             )
+            nc.vector.tensor_copy(v_g[:], tab_s[:].bitcast(U8).indirect(idx[:]))
         late = ctx.enter_context(tc.tile_pool(name="late", bufs=1))
-        tab2_w = [late.tile([P, T2], I32, name="tab2_w%d" % a) for a in range(PASSES)]
-        wl_raw = {
-            (g, a): late.tile([P, PACK, K_PASS], F32, name="wl_raw%d%d" % (g, a), tag="wl_raw%d%d" % (g, a), align_bytes=64)
-            for g in range(2)
-            for a in range(PASSES)
-        }
-        load_wl(0, 0)
-        load_tab2_scale_rows(0, 0)
-        load_tab2_scale_rows(1, 0)
-        load_tab2_scale_rows(0, 1)
-        load_tab2_scale_rows(1, 1)
-        load_wl(0, 1)
-        load_tab2_scale_rows(0, 2)
-        load_tab2_scale_rows(1, 2)
-        load_tab2_scale_rows(0, 3)
-        load_tab2_scale_rows(1, 3)
-        load_wl(1, 0)
-        load_wl(1, 1)
-        load_words(tab2_w[0], tab2_words[0])
-        load_words(tab2_w[1], tab2_words[1])
+        for g, a in ((0, 1), (1, 0), (1, 1)):
+            wl_raw.setdefault(
+                (g, a), late.tile([P, PACK, K_PASS], F32, name="wl_raw%d%d" % (g, a), tag="wl_raw%d%d" % (g, a), align_bytes=64)
+            )
+        for q in range(QUADS):
+            move_scale_rows(v_s, 0, v_g, q)
+        for g, a in ((0, 1), (1, 0), (1, 1)):
+            load_wl(g, a)
         nc.tensor.transpose(banks[7][:, 0:P], bc_rows[:], ident[:])
         nc.scalar.activation(bc_col[:], banks[7][:, 0 : S2 // P], ACT.Copy)
+        v_c = [tile([P, S], U32, "v_c%d" % a) for a in range(PASSES)]
+        nc.vector.tensor_copy(v_c[0][:], tab_w[0][:].bitcast(U32).indirect(idx[:]))
         nc.vector.tensor_copy(
             ws_s[:].rearrange("p (b t m) -> p b t m", t=PACK, m=P),
             ws_sraw[:].rearrange("p a c -> p (a c)").bitcast(U8).rearrange("p (b m t) -> p b t m", t=PACK, m=P),
         )
-
-        v_c = [tile([P, S], U32, "v_c%d" % a) for a in range(PASSES)]
-        v_s = [tile([P, S], U8, "v_s%d" % a) for a in range(PASSES)]
+        nc.vector.tensor_copy(v_c[1][:], tab_w[1][:].bitcast(U32).indirect(idx[:]))
+        nc.vector.tensor_copy(v2_g[:], tab2_s[:].bitcast(U8).indirect(idx2[:]))
+        for q in range(QUADS):
+            move_scale_rows(v2_s, V2_ROW, v2_g, q)
+        tab2_w = [tile([P, T2], I32, "tab2_w%d" % a, ("tab2_s", "v2_g")[a]) for a in range(PASSES)]
         for a in range(PASSES):
-            nc.vector.tensor_copy(v_c[a][:], tab_w[a][:].bitcast(U32).indirect(idx[:]))
-            nc.vector.tensor_copy(v_s[a][:], tab_s[:, a, :].bitcast(U8).indirect(idx[:]))
+            load_words(tab2_w[a], tab2_words[a])
 
-        def short_term(g):
-            for a in range(PASSES):
+        def short_term(g, passes):
+            for a in passes:
                 for t in range(PACK):
                     col = ((a * 2 + g) * PACK + t) * P
                     nc.tensor.matmul_mx(
@@ -154,7 +157,7 @@ def tile_list_session_drift_novelty_kernel(
                         lhsT=ws_c[:, 2 * col : 2 * col + 2 * P].bitcast(FP4X4),
                         lhsT_scale=ws_s[:, col : col + P],
                         rhs=v_c[a][:].bitcast(FP8X4),
-                        rhs_scale=v_s[a][:],
+                        rhs_scale=v_s[:, a, :].bitcast(U8),
                         start=(a == 0),
                         stop=False,
                     )
@@ -171,7 +174,8 @@ def tile_list_session_drift_novelty_kernel(
             src = raw[:].rearrange("p j (m t) -> p m t j", t=PACK)
             dst = neg[:].rearrange("p t m j -> p m t j")
             cut = M_VEC[g, a]
-            nc.scalar.activation(dst[:, cut:P], src[:, cut:P], ACT.Copy, scale=-1.0)
+            if cut < P:
+                nc.scalar.activation(dst[:, cut:P], src[:, cut:P], ACT.Copy, scale=-1.0)
             if cut:
                 nc.vector.tensor_scalar(dst[:, 0:cut], src[:, 0:cut], -1.0, None, ALU.mult)
             nc.vector.quantize_mx(
@@ -183,7 +187,7 @@ def tile_list_session_drift_novelty_kernel(
                     lhsT=codes[:, t * P : (t + 1) * P].bitcast(FP8X4),
                     lhsT_scale=scales[:, t * P : (t + 1) * P],
                     rhs=v_c[a][:].bitcast(FP8X4),
-                    rhs_scale=v_s[a][:],
+                    rhs_scale=v_s[:, a, :].bitcast(U8),
                     start=False,
                     stop=(a == PASSES - 1),
                 )
@@ -208,20 +212,19 @@ def tile_list_session_drift_novelty_kernel(
             nc.tensor.matmul_mx(
                 out=banks[u][:],
                 lhsT=v2_c[a][:, u * P : (u + 1) * P].bitcast(FP8X4),
-                lhsT_scale=v2_s[V2_ROW[a] : P, u * P : (u + 1) * P],
+                lhsT_scale=v2_s[V2_ROW:P, a, u * P // 4 : (u + 1) * P // 4].bitcast(U8),
                 rhs=h_c[a][:].bitcast(FP8X4),
                 rhs_scale=h_s[a][:],
                 start=(a == 0),
                 stop=(a == PASSES - 1),
             )
 
-        short_term(0)
+        short_term(0, (0, 1))
         quantise_wl(0, 0)
         quantise_wl(0, 1)
-        v2_s = tile([P, S2], U8, "v2_s", "neg01")
-        nc.vector.tensor_copy(v2_s[:], tab2_s[:].bitcast(U8).indirect(idx2[:]))
-        short_term(1)
+        short_term(1, (0,))
         quantise_wl(1, 0)
+        short_term(1, (1,))
         quantise_wl(1, 1)
         drift(0)
         drift(1)

@@ -194,7 +194,7 @@ def tile_list_session_drift_novelty_kernel(
 
         def drift(g):
             planes = late.tile([P, PACK, S], BF16, name="planes%d" % g, tag=("wl_raw10", "planes1")[g], align_bytes=64)
-            packed = tile([P, S, PACK], BF16, "packed%d" % g, "packed%d" % g)
+            packed = tile([P, S, PACK], BF16, "packed%d" % g, ("packed0", "tab2_s")[g])
             for t in range(PACK):
                 nc.scalar.activation(planes[:, t, :], banks[g * PACK + t][:], ACT.Abs, bias=bd_col[:, g, t : t + 1])
             nc.vector.tensor_copy(packed[:], planes[:].rearrange("p t n -> p n t"))
@@ -227,13 +227,13 @@ def tile_list_session_drift_novelty_kernel(
         short_term(1, (1,))
         quantise_wl(1, 1)
         drift(0)
-        drift(1)
         v2_c.append(tile([P, S2], U32, "v2_c0", "packed0"))
         for c in range(S2 // GATHER):
             gather_v2(0, c)
+        drift(1)
         for u in range(S2 // P):
             score_pass(0, u)
-        v2_c.append(tile([P, S2], U32, "v2_c1", "packed1"))
+        v2_c.append(tile([P, S2], U32, "v2_c1", "tab2_s"))
         for c in range(S2 // GATHER):
             gather_v2(1, c)
         for u in range(S2 // P):

@@ -22,8 +22,12 @@ PACK = 4
 K_PASS = P * PACK
 PASSES = 2
 QUADS = 4
+QUAD = P // QUADS
+ROWS = 4
+WORD = 4
+BANKS = 8
 V2_ROW = 4
-M_VEC = {(0, 0): 0, (0, 1): 64, (1, 0): 64, (1, 1): 128}
+VECTOR_COLUMNS = {(0, 0): 0, (0, 1): 64, (1, 0): 64, (1, 1): 128}
 GATHER = 512
 
 
@@ -33,24 +37,28 @@ def tile_list_session_drift_novelty_kernel(
     nc = tc.nc
     with ExitStack() as ctx:
         keep = ctx.enter_context(tc.tile_pool(name="keep", bufs=1))
+        shared = ctx.enter_context(tc.tile_pool(name="shared", bufs=1))
         psum = ctx.enter_context(tc.psum_pool(name="psum", bufs=1))
 
         def tile(shape, dtype, name, tag=""):
             return keep.tile(shape, dtype, name=name, tag=tag, align_bytes=64)
 
+        def shared_tile(shape, dtype, name, offset):
+            return shared.tile(shape, dtype, name=name, offset=offset, align_bytes=64)
+
         idx = keep.tile([P, S // 16], U16, name="idx")
         idx2 = keep.tile([P, S2 // 16], U16, name="idx2")
-        ws_sraw = tile([P, PASSES, H // 4], I32, "ws_sraw")
-        ws_raw = tile([P, PASSES, H // 2], I32, "ws_raw")
-        v_s = tile([P, PASSES, S // 4], I32, "v_s")
-        v2_s = tile([P, PASSES, S2 // 4], I32, "v2_s")
+        ws_sraw = tile([P, PASSES, H // WORD], I32, "ws_sraw")
+        ws_raw = tile([P, PASSES, 2 * H // WORD], I32, "ws_raw")
+        v_s = tile([P, PASSES, S // WORD], I32, "v_s")
+        v2_s = tile([P, PASSES, S2 // WORD], I32, "v2_s")
         v_g = tile([P, S], U8, "v_g")
         v2_g = tile([P, S2], U8, "v2_g", "v2_g")
-        tab2_s = tile([P, T2 // 4], I32, "tab2_s", "tab2_s")
-        banks = [psum.tile([P, S], F32, name="bank%d" % b) for b in range(8)]
+        tab2_s = shared_tile([P, T2 // WORD], I32, "tab2_s", 0)
+        banks = [psum.tile([P, S], F32, name="bank%d" % b) for b in range(BANKS)]
 
         ident = tile([P, P], F32, "ident")
-        bd_col = tile([P, 2, PACK], F32, "bd_col")
+        bd_col = tile([P, PASSES, PACK], F32, "bd_col")
         bc_col = tile([P, S2 // P], F32, "bc_col")
         with tc.tile_pool(name="warm", bufs=1) as warm_pool:
             warm_in = warm_pool.tile([P, 8], F32, name="warm_in")
@@ -62,29 +70,12 @@ def tile_list_session_drift_novelty_kernel(
         bc_rows = tile([P, P], F32, "bc_rows")
         wl_raw = {(0, 0): mid.tile([P, PACK, K_PASS], F32, name="wl_raw00")}
 
-        def load_idx():
-            nc.sync.dma_start(idx[:], offs)
-
-        def load_idx2():
-            nc.sync.dma_start(idx2[:], offs2)
-
-        def load_bc():
-            nc.sync.dma_start(bc_rows[0 : S2 // P, :], bc.rearrange("(u m) -> u m", m=P))
-
-        def load_bd():
-            nc.sync.dma_start(bd_col[:], bd.rearrange("(g p t) -> p g t", g=2, t=PACK))
-
-        def load_ws():
-            nc.sync.dma_start(ws_raw[:], ws_words.rearrange("a p c -> p a c").bitcast(I32))
-
-        def load_scale_rows(dst, src, r):
-            nc.sync.dma_start(dst[r:P:32, :, :], src[:, r:16:4, :].rearrange("a q c -> q a c").bitcast(I32))
-
         def load_scale_table(dst, src):
             nc.sync.dma_start(dst[0:P:4, :], src.rearrange("a q c -> q a c").bitcast(I32))
 
-        def move_scale_rows(dst, row, src, q):
-            nc.sync.dma_start(dst[32 * q + row : 32 * q + row + 4, :, :], src[32 * q : 32 * q + 32 : 4, :].bitcast(I32))
+        def move_scale_rows(dst, row, src, quad):
+            first = QUAD * quad
+            nc.sync.dma_start(dst[first + row : first + row + ROWS, :, :], src[first : first + QUAD : 4, :].bitcast(I32))
 
         def load_words(dst, src):
             nc.sync.dma_start(dst[:], src.rearrange("p t i -> p (t i)").bitcast(I32))
@@ -97,8 +88,8 @@ def tile_list_session_drift_novelty_kernel(
 
         ws_c = tile([P, PASSES * H * 2], U8, "ws_c")
         ws_s = tile([P, PASSES * H], U8, "ws_s")
-        with tc.tile_pool(name="first", bufs=1) as first:
-            tab_s = first.tile([P, T // 4], I32, name="tab_s")
+        with tc.tile_pool(name="first", bufs=1) as first_pool:
+            tab_s = first_pool.tile([P, T // WORD], I32, name="tab_s")
             nc.vector.memset(tab_s[:], 0)
             nc.vector.memset(tab2_s[:], 0)
             nc.gpsimd.memset(ws_sraw[:], 0)
@@ -106,16 +97,19 @@ def tile_list_session_drift_novelty_kernel(
             make_identity(nc, ident[:])
             nc.gpsimd.memset(v2_s[:], 0)
             nc.gpsimd.memset(bc_rows[:], 0.0)
-            load_ws()
-            load_idx()
-            load_idx2()
-            load_bd()
+            nc.sync.dma_start(ws_raw[:], ws_words.rearrange("a p c -> p a c").bitcast(I32))
+            nc.sync.dma_start(idx[:], offs)
+            nc.sync.dma_start(idx2[:], offs2)
+            nc.sync.dma_start(bd_col[:], bd.rearrange("(g p t) -> p g t", g=PASSES, t=PACK))
             load_words(tab_w[0], tab_words[0])
             load_scale_table(tab_s, tab_scales)
-            for r in range(4):
-                load_scale_rows(ws_sraw, ws_scales, r)
+            for s in range(ROWS):
+                nc.sync.dma_start(
+                    ws_sraw[s:P:QUAD, :, :],
+                    ws_scales[:, s : QUADS * ROWS : ROWS, :].rearrange("a q c -> q a c").bitcast(I32),
+                )
             load_scale_table(tab2_s, tab2_scales)
-            load_bc()
+            nc.sync.dma_start(bc_rows[0 : S2 // P, :], bc.rearrange("(u m) -> u m", m=P))
             load_words(tab_w[1], tab_words[1])
             load_wl(0, 0)
             nc.vector.tensor_copy(
@@ -124,16 +118,16 @@ def tile_list_session_drift_novelty_kernel(
             )
             nc.vector.tensor_copy(v_g[:], tab_s[:].bitcast(U8).indirect(idx[:]))
         late = ctx.enter_context(tc.tile_pool(name="late", bufs=1))
-        for g, a in ((0, 1), (1, 0), (1, 1)):
-            wl_raw.setdefault(
-                (g, a), late.tile([P, PACK, K_PASS], F32, name="wl_raw%d%d" % (g, a), tag="wl_raw%d%d" % (g, a), align_bytes=64)
-            )
-        for q in range(QUADS):
-            move_scale_rows(v_s, 0, v_g, q)
-        for g, a in ((0, 1), (1, 0), (1, 1)):
+        late_chunks = ((0, 1), (1, 0), (1, 1))
+        for g, a in late_chunks:
+            name = "wl_raw%d%d" % (g, a)
+            wl_raw.setdefault((g, a), late.tile([P, PACK, K_PASS], F32, name=name, tag=name, align_bytes=64))
+        for quad in range(QUADS):
+            move_scale_rows(v_s, 0, v_g, quad)
+        for g, a in late_chunks:
             load_wl(g, a)
-        nc.tensor.transpose(banks[7][:, 0:P], bc_rows[:], ident[:])
-        nc.scalar.activation(bc_col[:], banks[7][:, 0 : S2 // P], ACT.Copy)
+        nc.tensor.transpose(banks[BANKS - 1][:, 0:P], bc_rows[:], ident[:])
+        nc.scalar.activation(bc_col[:], banks[BANKS - 1][:, 0 : S2 // P], ACT.Copy)
         v_c = [tile([P, S], U32, "v_c%d" % a) for a in range(PASSES)]
         nc.vector.tensor_copy(v_c[0][:], tab_w[0][:].bitcast(U32).indirect(idx[:]))
         nc.vector.tensor_copy(
@@ -142,38 +136,36 @@ def tile_list_session_drift_novelty_kernel(
         )
         nc.vector.tensor_copy(v_c[1][:], tab_w[1][:].bitcast(U32).indirect(idx[:]))
         nc.vector.tensor_copy(v2_g[:], tab2_s[:].bitcast(U8).indirect(idx2[:]))
-        for q in range(QUADS):
-            move_scale_rows(v2_s, V2_ROW, v2_g, q)
-        tab2_w = [tile([P, T2], I32, "tab2_w%d" % a, ("tab2_s", "v2_g")[a]) for a in range(PASSES)]
+        for quad in range(QUADS):
+            move_scale_rows(v2_s, V2_ROW, v2_g, quad)
+        tab2_w = [shared_tile([P, T2], I32, "tab2_w0", 0), tile([P, T2], I32, "tab2_w1", "v2_g")]
         for a in range(PASSES):
             load_words(tab2_w[a], tab2_words[a])
 
-        def short_term(g, passes):
-            for a in passes:
-                for t in range(PACK):
-                    col = ((a * 2 + g) * PACK + t) * P
-                    nc.tensor.matmul_mx(
-                        out=banks[g * PACK + t][:],
-                        lhsT=ws_c[:, 2 * col : 2 * col + 2 * P].bitcast(FP4X4),
-                        lhsT_scale=ws_s[:, col : col + P],
-                        rhs=v_c[a][:].bitcast(FP8X4),
-                        rhs_scale=v_s[:, a, :].bitcast(U8),
-                        start=(a == 0),
-                        stop=False,
-                    )
+        def add_short_term(g, a):
+            for t in range(PACK):
+                col = ((a * 2 + g) * PACK + t) * P
+                nc.tensor.matmul_mx(
+                    out=banks[g * PACK + t][:],
+                    lhsT=ws_c[:, 2 * col : 2 * col + 2 * P].bitcast(FP4X4),
+                    lhsT_scale=ws_s[:, col : col + P],
+                    rhs=v_c[a][:].bitcast(FP8X4),
+                    rhs_scale=v_s[:, a, :].bitcast(U8),
+                    start=(a == 0),
+                    stop=False,
+                )
 
         v2_c = []
-        h_c = [tile([P, S], U32, "h_c%d" % g) for g in range(2)]
-        h_s = [tile([P, S], U8, "h_s%d" % g) for g in range(2)]
+        h_c = []
+        h_s = [tile([P, S], U8, "h_s%d" % g) for g in range(PASSES)]
 
-        def quantise_wl(g, a):
-            raw = wl_raw[g, a]
+        def subtract_long_term(g, a):
             neg = tile([P, PACK, P, PACK], BF16, "neg%d%d" % (g, a), "neg%d%d" % (g, a))
             codes = tile([P, K_PASS], U32, "wl_c%d%d" % (g, a))
             scales = tile([P, K_PASS], U8, "wl_s%d%d" % (g, a))
-            src = raw[:].rearrange("p j (m t) -> p m t j", t=PACK)
+            src = wl_raw[g, a][:].rearrange("p j (m t) -> p m t j", t=PACK)
             dst = neg[:].rearrange("p t m j -> p m t j")
-            cut = M_VEC[g, a]
+            cut = VECTOR_COLUMNS[g, a]
             if cut < P:
                 nc.scalar.activation(dst[:, cut:P], src[:, cut:P], ACT.Copy, scale=-1.0)
             if cut:
@@ -192,52 +184,62 @@ def tile_list_session_drift_novelty_kernel(
                     stop=(a == PASSES - 1),
                 )
 
-        def drift(g):
-            planes = late.tile([P, PACK, S], BF16, name="planes%d" % g, tag=("wl_raw10", "planes1")[g], align_bytes=64)
-            packed = tile([P, S, PACK], BF16, "packed%d" % g, ("packed0", "tab2_s")[g])
+        def quantise_drift(g):
+            h_rows = late.tile([P, PACK, S], BF16, name="planes%d" % g, tag=("wl_raw10", "planes1")[g], align_bytes=64)
+            half = S // 2
+            if g == 0:
+                packed_v = tile([P, half, PACK], BF16, "packed_v0", "packed0")
+                h_c.append(tile([P, S], U32, "h_c0"))
+            else:
+                packed_v = shared_tile([P, half, PACK], BF16, "packed_v1", 0)
+                h_c.append(shared_tile([P, S], U32, "h_c1", WORD * S2))
+            packed_s = tile([P, half, PACK], BF16, "packed_s%d" % g)
             for t in range(PACK):
-                nc.scalar.activation(planes[:, t, :], banks[g * PACK + t][:], ACT.Abs, bias=bd_col[:, g, t : t + 1])
-            nc.vector.tensor_copy(packed[:], planes[:].rearrange("p t n -> p n t"))
-            nc.vector.quantize_mx(
-                out=h_c[g][:].bitcast(FP8X4), scales=h_s[g][:], in_=packed[:].rearrange("p n t -> p (n t)")
-            )
+                nc.scalar.activation(h_rows[:, t, :], banks[g * PACK + t][:], ACT.Abs, bias=bd_col[:, g, t : t + 1])
+            nc.scalar.copy(packed_s[:], h_rows[:, :, half:S].rearrange("p t n -> p n t"))
+            nc.vector.tensor_copy(packed_v[:], h_rows[:, :, 0:half].rearrange("p t n -> p n t"))
+            for packed, n0 in ((packed_s, half), (packed_v, 0)):
+                nc.vector.quantize_mx(
+                    out=h_c[g][:, n0 : n0 + half].bitcast(FP8X4),
+                    scales=h_s[g][:, n0 : n0 + half],
+                    in_=packed[:].rearrange("p n t -> p (n t)"),
+                )
 
-        def gather_v2(a, c):
-            nc.vector.tensor_copy(
-                v2_c[a][:, c * GATHER : (c + 1) * GATHER],
-                tab2_w[a][:].bitcast(U32).indirect(idx2[:, c * GATHER // 16 : (c + 1) * GATHER // 16]),
-            )
+        def gather_v2(a):
+            for c in range(S2 // GATHER):
+                nc.vector.tensor_copy(
+                    v2_c[a][:, c * GATHER : (c + 1) * GATHER],
+                    tab2_w[a][:].bitcast(U32).indirect(idx2[:, c * GATHER // 16 : (c + 1) * GATHER // 16]),
+                )
 
-        def score_pass(a, u):
+        def add_scores(a, u):
             nc.tensor.matmul_mx(
                 out=banks[u][:],
                 lhsT=v2_c[a][:, u * P : (u + 1) * P].bitcast(FP8X4),
-                lhsT_scale=v2_s[V2_ROW:P, a, u * P // 4 : (u + 1) * P // 4].bitcast(U8),
+                lhsT_scale=v2_s[V2_ROW:P, a, u * P // WORD : (u + 1) * P // WORD].bitcast(U8),
                 rhs=h_c[a][:].bitcast(FP8X4),
                 rhs_scale=h_s[a][:],
                 start=(a == 0),
                 stop=(a == PASSES - 1),
             )
 
-        short_term(0, (0, 1))
-        quantise_wl(0, 0)
-        quantise_wl(0, 1)
-        short_term(1, (0,))
-        quantise_wl(1, 0)
-        short_term(1, (1,))
-        quantise_wl(1, 1)
-        drift(0)
+        add_short_term(0, 0)
+        add_short_term(0, 1)
+        subtract_long_term(0, 0)
+        subtract_long_term(0, 1)
+        for a in range(PASSES):
+            add_short_term(1, a)
+            subtract_long_term(1, a)
+        quantise_drift(0)
         v2_c.append(tile([P, S2], U32, "v2_c0", "packed0"))
-        for c in range(S2 // GATHER):
-            gather_v2(0, c)
-        drift(1)
+        gather_v2(0)
+        quantise_drift(1)
         for u in range(S2 // P):
-            score_pass(0, u)
-        v2_c.append(tile([P, S2], U32, "v2_c1", "tab2_s"))
-        for c in range(S2 // GATHER):
-            gather_v2(1, c)
+            add_scores(0, u)
+        v2_c.append(shared_tile([P, S2], U32, "v2_c1", 0))
+        gather_v2(1)
         for u in range(S2 // P):
-            score_pass(1, u)
+            add_scores(1, u)
             res = tile([P, S], F32, "res%d" % u)
             nc.scalar.activation(res[:], banks[u][:], ACT.Sigmoid, bias=bc_col[:, u : u + 1])
             nc.sync.dma_start(out[u * P : (u + 1) * P, :], res[:])

@@ -29,6 +29,7 @@ BANKS = 8
 V2_ROW = 4
 VECTOR_COLUMNS = {(0, 0): 0, (0, 1): 64, (1, 0): 64, (1, 1): 128}
 GATHER = 512
+RUN = 4
 
 
 def tile_list_session_drift_novelty_kernel(
@@ -163,8 +164,8 @@ def tile_list_session_drift_novelty_kernel(
             neg = tile([P, PACK, P, PACK], BF16, "neg%d%d" % (g, a), "neg%d%d" % (g, a))
             codes = tile([P, K_PASS], U32, "wl_c%d%d" % (g, a))
             scales = tile([P, K_PASS], U8, "wl_s%d%d" % (g, a))
-            src = wl_raw[g, a][:].rearrange("p j (m t) -> p m t j", t=PACK)
-            dst = neg[:].rearrange("p t m j -> p m t j")
+            src = wl_raw[g, a][:].rearrange("p j (m t) -> p m j t", t=PACK)
+            dst = neg[:].rearrange("p t m j -> p m j t")
             cut = VECTOR_COLUMNS[g, a]
             if cut < P:
                 nc.scalar.activation(dst[:, cut:P], src[:, cut:P], ACT.Copy, scale=-1.0)
@@ -196,8 +197,14 @@ def tile_list_session_drift_novelty_kernel(
             packed_s = tile([P, half, PACK], BF16, "packed_s%d" % g)
             for t in range(PACK):
                 nc.scalar.activation(h_rows[:, t, :], banks[g * PACK + t][:], ACT.Abs, bias=bd_col[:, g, t : t + 1])
-            nc.scalar.copy(packed_s[:], h_rows[:, :, half:S].rearrange("p t n -> p n t"))
-            nc.vector.tensor_copy(packed_v[:], h_rows[:, :, 0:half].rearrange("p t n -> p n t"))
+            nc.scalar.copy(
+                packed_s[:].rearrange("p (c i) t -> p c t i", i=RUN),
+                h_rows[:, :, half:S].rearrange("p t (c i) -> p c t i", i=RUN),
+            )
+            nc.vector.tensor_copy(
+                packed_v[:].rearrange("p (c i) t -> p c t i", i=RUN),
+                h_rows[:, :, 0:half].rearrange("p t (c i) -> p c t i", i=RUN),
+            )
             for packed, n0 in ((packed_s, half), (packed_v, 0)):
                 nc.vector.quantize_mx(
                     out=h_c[g][:, n0 : n0 + half].bitcast(FP8X4),

@@ -29,6 +29,8 @@ BANKS = 8
 V2_ROW = 4
 VECTOR_COLUMNS = {(0, 0): 0, (0, 1): 64, (1, 0): 64, (1, 1): 128}
 GATHER = 512
+ALIGN = 256
+QUAD_ORDER = (0, 2, 1, 3)
 RUN = 4
 
 
@@ -42,10 +44,10 @@ def tile_list_session_drift_novelty_kernel(
         psum = ctx.enter_context(tc.psum_pool(name="psum", bufs=1))
 
         def tile(shape, dtype, name, tag=""):
-            return keep.tile(shape, dtype, name=name, tag=tag, align_bytes=64)
+            return keep.tile(shape, dtype, name=name, tag=tag, align_bytes=ALIGN)
 
         def shared_tile(shape, dtype, name, offset):
-            return shared.tile(shape, dtype, name=name, offset=offset, align_bytes=64)
+            return shared.tile(shape, dtype, name=name, offset=offset, align_bytes=ALIGN)
 
         idx = keep.tile([P, S // 16], U16, name="idx")
         idx2 = keep.tile([P, S2 // 16], U16, name="idx2")
@@ -67,9 +69,9 @@ def tile_list_session_drift_novelty_kernel(
             nc.gpsimd.memset(warm_in[:], 0.0)
             nc.scalar.activation(warm[:], warm_in[:], ACT.Sigmoid)
         mid = ctx.enter_context(tc.tile_pool(name="mid", bufs=1))
-        tab_w = [tile([P, T], I32, "tab_w0"), mid.tile([P, T], I32, name="tab_w1")]
+        tab_w = [tile([P, T], I32, "tab_w0"), mid.tile([P, T], I32, name="tab_w1", align_bytes=ALIGN)]
         bc_rows = tile([P, P], F32, "bc_rows")
-        wl_raw = {(0, 0): mid.tile([P, PACK, K_PASS], F32, name="wl_raw00")}
+        wl_raw = {(0, 0): mid.tile([P, PACK, K_PASS], F32, name="wl_raw00", align_bytes=ALIGN)}
 
         def load_scale_table(dst, src):
             nc.sync.dma_start(dst[0:P:4, :], src.rearrange("a q c -> q a c").bitcast(I32))
@@ -90,7 +92,7 @@ def tile_list_session_drift_novelty_kernel(
         ws_c = tile([P, PASSES * H * 2], U8, "ws_c")
         ws_s = tile([P, PASSES * H], U8, "ws_s")
         with tc.tile_pool(name="first", bufs=1) as first_pool:
-            tab_s = first_pool.tile([P, T // WORD], I32, name="tab_s")
+            tab_s = first_pool.tile([P, T // WORD], I32, name="tab_s", align_bytes=ALIGN)
             nc.vector.memset(tab_s[:], 0)
             nc.vector.memset(tab2_s[:], 0)
             nc.gpsimd.memset(ws_sraw[:], 0)
@@ -122,8 +124,8 @@ def tile_list_session_drift_novelty_kernel(
         late_chunks = ((0, 1), (1, 0), (1, 1))
         for g, a in late_chunks:
             name = "wl_raw%d%d" % (g, a)
-            wl_raw.setdefault((g, a), late.tile([P, PACK, K_PASS], F32, name=name, tag=name, align_bytes=64))
-        for quad in range(QUADS):
+            wl_raw.setdefault((g, a), late.tile([P, PACK, K_PASS], F32, name=name, tag=name, align_bytes=ALIGN))
+        for quad in QUAD_ORDER:
             move_scale_rows(v_s, 0, v_g, quad)
         for g, a in late_chunks:
             load_wl(g, a)
@@ -137,7 +139,7 @@ def tile_list_session_drift_novelty_kernel(
         )
         nc.vector.tensor_copy(v_c[1][:], tab_w[1][:].bitcast(U32).indirect(idx[:]))
         nc.vector.tensor_copy(v2_g[:], tab2_s[:].bitcast(U8).indirect(idx2[:]))
-        for quad in range(QUADS):
+        for quad in QUAD_ORDER:
             move_scale_rows(v2_s, V2_ROW, v2_g, quad)
         tab2_w = [shared_tile([P, T2], I32, "tab2_w0", 0), tile([P, T2], I32, "tab2_w1", "v2_g")]
         for a in range(PASSES):
@@ -186,7 +188,7 @@ def tile_list_session_drift_novelty_kernel(
                 )
 
         def quantise_drift(g):
-            h_rows = late.tile([P, PACK, S], BF16, name="planes%d" % g, tag=("wl_raw10", "planes1")[g], align_bytes=64)
+            h_rows = late.tile([P, PACK, S], BF16, name="planes%d" % g, tag=("wl_raw10", "planes1")[g], align_bytes=ALIGN)
             half = S // 2
             if g == 0:
                 packed_v = tile([P, half, PACK], BF16, "packed_v0", "packed0")

@@ -56,8 +56,8 @@ def tile_list_session_drift_novelty_kernel(
         v_s = tile([P, PASSES, S // WORD], I32, "v_s")
         v2_s = tile([P, PASSES, S2 // WORD], I32, "v2_s")
         v_g = tile([P, S], U8, "v_g")
-        v2_g = tile([P, S2], U8, "v2_g", "v2_g")
-        tab2_s = shared_tile([P, T2 // WORD], I32, "tab2_s", 0)
+        v2_g = tile([P, S2], U8, "v2_g")
+        tab2_s = shared_tile([P, T2 // WORD], I32, "tab2_s", WORD * T2 - T2 // 2)
         banks = [psum.tile([P, S], F32, name="bank%d" % b) for b in range(BANKS)]
 
         ident = tile([P, P], F32, "ident")
@@ -139,14 +139,23 @@ def tile_list_session_drift_novelty_kernel(
         )
         nc.vector.tensor_copy(v_c[1][:], tab_w[1][:].bitcast(U32).indirect(idx[:]))
         nc.vector.tensor_copy(v2_g[:], tab2_s[:].bitcast(U8).indirect(idx2[:]))
-        for quad in QUAD_ORDER:
-            move_scale_rows(v2_s, V2_ROW, v2_g, quad)
-        tab2_w = [shared_tile([P, T2], I32, "tab2_w0", 0), tile([P, T2], I32, "tab2_w1", "v2_g")]
+
+        def move_v2_scale_rows(a):
+            for quad in QUAD_ORDER:
+                first = QUAD * quad
+                nc.sync.dma_start(
+                    v2_s[first + V2_ROW : first + V2_ROW + ROWS, a, :],
+                    v2_g[first + 4 * a : first + QUAD : 8, :].bitcast(I32),
+                )
+
+        tab2_w = [shared_tile([P, T2], I32, "tab2_w%d" % a, a * WORD * T2) for a in range(PASSES)]
+        move_v2_scale_rows(0)
         for a in range(PASSES):
             load_words(tab2_w[a], tab2_words[a])
+        move_v2_scale_rows(1)
 
-        def add_short_term(g, a):
-            for t in range(PACK):
+        def add_short_term(g, a, slots=range(PACK)):
+            for t in slots:
                 col = ((a * 2 + g) * PACK + t) * P
                 nc.tensor.matmul_mx(
                     out=banks[g * PACK + t][:],
@@ -154,7 +163,7 @@ def tile_list_session_drift_novelty_kernel(
                     lhsT_scale=ws_s[:, col : col + P],
                     rhs=v_c[a][:].bitcast(FP8X4),
                     rhs_scale=v_s[:, a, :].bitcast(U8),
-                    start=(a == 0),
+                    start=(g, a) == (0, 0),
                     stop=False,
                 )
 
@@ -163,7 +172,8 @@ def tile_list_session_drift_novelty_kernel(
         h_s = [tile([P, S], U8, "h_s%d" % g) for g in range(PASSES)]
 
         def subtract_long_term(g, a):
-            neg = tile([P, PACK, P, PACK], BF16, "neg%d%d" % (g, a), "neg%d%d" % (g, a))
+            name = "neg%d%d" % (g, a)
+            neg = tile([P, PACK, P, PACK], BF16, name, "packed0" if (g, a) == (1, 1) else name)
             codes = tile([P, K_PASS], U32, "wl_c%d%d" % (g, a))
             scales = tile([P, K_PASS], U8, "wl_s%d%d" % (g, a))
             src = wl_raw[g, a][:].rearrange("p j (m t) -> p m j t", t=PACK)
@@ -177,13 +187,15 @@ def tile_list_session_drift_novelty_kernel(
                 out=codes[:].bitcast(FP8X4), scales=scales[:], in_=neg[:].rearrange("p t m j -> p (t m j)")
             )
             for t in range(PACK):
+                if (g, a) == (1, 1):
+                    add_short_term(g, a, (t,))
                 nc.tensor.matmul_mx(
                     out=banks[g * PACK + t][:],
                     lhsT=codes[:, t * P : (t + 1) * P].bitcast(FP8X4),
                     lhsT_scale=scales[:, t * P : (t + 1) * P],
                     rhs=v_c[a][:].bitcast(FP8X4),
                     rhs_scale=v_s[:, a, :].bitcast(U8),
-                    start=False,
+                    start=(g, a) == (1, 0),
                     stop=(a == PASSES - 1),
                 )
 
@@ -236,9 +248,9 @@ def tile_list_session_drift_novelty_kernel(
         add_short_term(0, 1)
         subtract_long_term(0, 0)
         subtract_long_term(0, 1)
-        for a in range(PASSES):
-            add_short_term(1, a)
-            subtract_long_term(1, a)
+        subtract_long_term(1, 0)
+        add_short_term(1, 0)
+        subtract_long_term(1, 1)
         quantise_drift(0)
         v2_c.append(tile([P, S2], U32, "v2_c0", "packed0"))
         gather_v2(0)

@@ -1,7 +1,6 @@
 from contextlib import ExitStack
 
 import concourse.mybir as mybir
-from concourse.masks import make_identity
 
 K, H, T, S, T2, S2 = 1024, 1024, 2048, 512, 4096, 1024
 FLOPS = 2 * (2 * K * H * S + H * S2 * S)
@@ -27,7 +26,7 @@ ROWS = 4
 WORD = 4
 BANKS = 8
 V2_ROW = 4
-VECTOR_COLUMNS = {(0, 0): 0, (0, 1): 64, (1, 0): 64, (1, 1): 128}
+VECTOR_COLUMNS = {(0, 0): 0, (0, 1): 96, (1, 0): 128, (1, 1): 128}
 GATHER = 512
 ALIGN = 256
 QUAD_ORDER = (0, 2, 1, 3)
@@ -51,27 +50,40 @@ def tile_list_session_drift_novelty_kernel(
 
         idx = keep.tile([P, S // 16], U16, name="idx")
         idx2 = keep.tile([P, S2 // 16], U16, name="idx2")
-        ws_sraw = tile([P, PASSES, H // WORD], I32, "ws_sraw")
+        head = ctx.enter_context(tc.tile_pool(name="head", bufs=1))
+        ws_sraw = head.tile([P, PASSES, H // WORD], I32, name="ws_sraw", offset=WORD * T, align_bytes=ALIGN)
         ws_raw = tile([P, PASSES, 2 * H // WORD], I32, "ws_raw")
         v_s = tile([P, PASSES, S // WORD], I32, "v_s")
         v2_s = tile([P, PASSES, S2 // WORD], I32, "v2_s")
-        v_g = tile([P, S], U8, "v_g")
-        v2_g = tile([P, S2], U8, "v2_g")
         tab2_s = shared_tile([P, T2 // WORD], I32, "tab2_s", WORD * T2 - T2 // 2)
         banks = [psum.tile([P, S], F32, name="bank%d" % b) for b in range(BANKS)]
 
         ident = tile([P, P], F32, "ident")
-        bd_col = tile([P, PASSES, PACK], F32, "bd_col")
         bc_col = tile([P, S2 // P], F32, "bc_col")
-        with tc.tile_pool(name="warm", bufs=1) as warm_pool:
-            warm_in = warm_pool.tile([P, 8], F32, name="warm_in")
-            warm = warm_pool.tile([P, 8], F32, name="warm")
-            nc.gpsimd.memset(warm_in[:], 0.0)
-            nc.scalar.activation(warm[:], warm_in[:], ACT.Sigmoid)
-        mid = ctx.enter_context(tc.tile_pool(name="mid", bufs=1))
-        tab_w = [tile([P, T], I32, "tab_w0"), mid.tile([P, T], I32, name="tab_w1", align_bytes=ALIGN)]
-        bc_rows = tile([P, P], F32, "bc_rows")
-        wl_raw = {(0, 0): mid.tile([P, PACK, K_PASS], F32, name="wl_raw00", align_bytes=ALIGN)}
+        chunk0 = WORD * T + WORD * H
+        warm_in = tile([P, 8], F32, "warm_in")
+        warm = tile([P, 8], F32, "warm")
+        nc.gpsimd.memset(warm_in[:], 0.0)
+        nc.scalar.activation(warm[:], warm_in[:], ACT.Sigmoid)
+        zeros = [
+            head.tile([P, P // 2], F32, name="zeros0", offset=0, align_bytes=ALIGN),
+            head.tile([P, P // 2], F32, name="zeros1", offset=chunk0 - P),
+        ]
+        for source in zeros:
+            nc.gpsimd.memset(source[:], 0.0)
+
+        def half_identity(c):
+            nc.gpsimd.affine_select(
+                out=ident[:, c * P // 2 : (c + 1) * P // 2],
+                in_=zeros[c][:],
+                compare_op=ALU.not_equal,
+                fill=1.0,
+                base=-c * P // 2,
+                pattern=[[-1, P // 2]],
+                channel_multiplier=1,
+            )
+
+        wl_raw = {}
 
         def load_scale_table(dst, src):
             nc.sync.dma_start(dst[0:P:4, :], src.rearrange("a q c -> q a c").bitcast(I32))
@@ -90,54 +102,60 @@ def tile_list_session_drift_novelty_kernel(
             )
 
         ws_c = tile([P, PASSES * H * 2], U8, "ws_c")
-        ws_s = tile([P, PASSES * H], U8, "ws_s")
         with tc.tile_pool(name="first", bufs=1) as first_pool:
             tab_s = first_pool.tile([P, T // WORD], I32, name="tab_s", align_bytes=ALIGN)
-            nc.vector.memset(tab_s[:], 0)
-            nc.vector.memset(tab2_s[:], 0)
+            nc.gpsimd.memset(tab_s[:], 0)
+            half_identity(0)
             nc.gpsimd.memset(ws_sraw[:], 0)
-            nc.gpsimd.memset(v_s[:], 0)
-            make_identity(nc, ident[:])
-            nc.gpsimd.memset(v2_s[:], 0)
-            nc.gpsimd.memset(bc_rows[:], 0.0)
+            nc.gpsimd.memset(tab2_s[:], 0)
+            half_identity(1)
+            nc.vector.memset(v_s[:], 0)
+            nc.vector.memset(v2_s[:], 0)
             nc.sync.dma_start(ws_raw[:], ws_words.rearrange("a p c -> p a c").bitcast(I32))
             nc.sync.dma_start(idx[:], offs)
             nc.sync.dma_start(idx2[:], offs2)
-            nc.sync.dma_start(bd_col[:], bd.rearrange("(g p t) -> p g t", g=PASSES, t=PACK))
-            load_words(tab_w[0], tab_words[0])
             load_scale_table(tab_s, tab_scales)
+            tab_w = [head.tile([P, T], I32, name="tab_w0", offset=0, align_bytes=ALIGN)]
+            load_words(tab_w[0], tab_words[0])
             for s in range(ROWS):
                 nc.sync.dma_start(
                     ws_sraw[s:P:QUAD, :, :],
                     ws_scales[:, s : QUADS * ROWS : ROWS, :].rearrange("a q c -> q a c").bitcast(I32),
                 )
             load_scale_table(tab2_s, tab2_scales)
-            nc.sync.dma_start(bc_rows[0 : S2 // P, :], bc.rearrange("(u m) -> u m", m=P))
-            load_words(tab_w[1], tab_words[1])
+            wl_raw.setdefault((0, 0), head.tile([P, PACK, K_PASS], F32, name="wl_raw00", offset=chunk0, align_bytes=ALIGN))
             load_wl(0, 0)
             nc.vector.tensor_copy(
                 ws_c[:].bitcast(U16).rearrange("p (b t m) -> p b t m", t=PACK, m=P),
                 ws_raw[:].rearrange("p a c -> p (a c)").bitcast(U16).rearrange("p (b m t) -> p b t m", t=PACK, m=P),
             )
+            v_g = head.tile([P, S], U8, name="v_g", offset=chunk0 - S, align_bytes=ALIGN)
             nc.vector.tensor_copy(v_g[:], tab_s[:].bitcast(U8).indirect(idx[:]))
         late = ctx.enter_context(tc.tile_pool(name="late", bufs=1))
+        ws_s = late.tile([P, PASSES * H], U8, name="ws_s", align_bytes=ALIGN)
         late_chunks = ((0, 1), (1, 0), (1, 1))
         for g, a in late_chunks:
             name = "wl_raw%d%d" % (g, a)
             wl_raw.setdefault((g, a), late.tile([P, PACK, K_PASS], F32, name=name, tag=name, align_bytes=ALIGN))
         for quad in QUAD_ORDER:
             move_scale_rows(v_s, 0, v_g, quad)
+        tab_w.append(late.tile([P, T], I32, name="tab_w1", align_bytes=ALIGN))
+        load_words(tab_w[1], tab_words[1])
+        bc_rows = late.tile([P, P], F32, name="bc_rows", align_bytes=ALIGN)
+        nc.gpsimd.memset(bc_rows[:], 0.0)
+        bd_col = late.tile([P, PASSES, 2 * PACK], F32, name="bd_col", align_bytes=ALIGN)
         for g, a in late_chunks:
             load_wl(g, a)
-        nc.tensor.transpose(banks[BANKS - 1][:, 0:P], bc_rows[:], ident[:])
-        nc.scalar.activation(bc_col[:], banks[BANKS - 1][:, 0 : S2 // P], ACT.Copy)
-        v_c = [tile([P, S], U32, "v_c%d" % a) for a in range(PASSES)]
+            if (g, a) == (0, 1):
+                nc.sync.dma_start(bd_col[:, :, 0:PACK], bd.rearrange("(g p t) -> p g t", g=PASSES, t=PACK))
+                nc.sync.dma_start(bc_rows[0 : S2 // P, :], bc.rearrange("(u m) -> u m", m=P))
+        v_c = [tile([P, S], U32, "v_c0")]
         nc.vector.tensor_copy(v_c[0][:], tab_w[0][:].bitcast(U32).indirect(idx[:]))
         nc.vector.tensor_copy(
             ws_s[:].rearrange("p (b t m) -> p b t m", t=PACK, m=P),
             ws_sraw[:].rearrange("p a c -> p (a c)").bitcast(U8).rearrange("p (b m t) -> p b t m", t=PACK, m=P),
         )
-        nc.vector.tensor_copy(v_c[1][:], tab_w[1][:].bitcast(U32).indirect(idx[:]))
+        v2_g = head.tile([P, S2], U8, name="v2_g", offset=WORD * T - S2 // 2, align_bytes=ALIGN)
         nc.vector.tensor_copy(v2_g[:], tab2_s[:].bitcast(U8).indirect(idx2[:]))
 
         def move_v2_scale_rows(a):
@@ -163,7 +181,7 @@ def tile_list_session_drift_novelty_kernel(
                     lhsT_scale=ws_s[:, col : col + P],
                     rhs=v_c[a][:].bitcast(FP8X4),
                     rhs_scale=v_s[:, a, :].bitcast(U8),
-                    start=(g, a) == (0, 0),
+                    start=(a == 0),
                     stop=False,
                 )
 
@@ -171,12 +189,15 @@ def tile_list_session_drift_novelty_kernel(
         h_c = []
         h_s = [tile([P, S], U8, "h_s%d" % g) for g in range(PASSES)]
 
-        def subtract_long_term(g, a):
-            name = "neg%d%d" % (g, a)
-            neg = tile([P, PACK, P, PACK], BF16, name, "packed0" if (g, a) == (1, 1) else name)
-            codes = tile([P, K_PASS], U32, "wl_c%d%d" % (g, a))
-            scales = tile([P, K_PASS], U8, "wl_s%d%d" % (g, a))
-            src = wl_raw[g, a][:].rearrange("p j (m t) -> p m j t", t=PACK)
+        def subtract_long_term(g, a, first=0, count=PACK):
+            name = "%d%d%d" % (g, a, first)
+            neg = tile([P, count, P, PACK], BF16, "neg" + name, "neg00" if (g, a) == (0, 0) else "packed0")
+            codes = tile([P, count * P], U32, "wl_c" + name)
+            if (g, a) == (0, 1):
+                scales = ws_s[ROWS:P, 3 * K_PASS : 4 * K_PASS]
+            else:
+                scales = tile([P, count * P], U8, "wl_s" + name)[:]
+            src = wl_raw[g, a][:].rearrange("p j (m t) -> p m j t", t=PACK)[:, :, :, first : first + count]
             dst = neg[:].rearrange("p t m j -> p m j t")
             cut = VECTOR_COLUMNS[g, a]
             if cut < P:
@@ -184,45 +205,52 @@ def tile_list_session_drift_novelty_kernel(
             if cut:
                 nc.vector.tensor_scalar(dst[:, 0:cut], src[:, 0:cut], -1.0, None, ALU.mult)
             nc.vector.quantize_mx(
-                out=codes[:].bitcast(FP8X4), scales=scales[:], in_=neg[:].rearrange("p t m j -> p (t m j)")
+                out=codes[:].bitcast(FP8X4), scales=scales, in_=neg[:].rearrange("p t m j -> p (t m j)")
             )
-            for t in range(PACK):
-                if (g, a) == (1, 1):
-                    add_short_term(g, a, (t,))
+            for t in range(count):
                 nc.tensor.matmul_mx(
-                    out=banks[g * PACK + t][:],
+                    out=banks[g * PACK + first + t][:],
                     lhsT=codes[:, t * P : (t + 1) * P].bitcast(FP8X4),
                     lhsT_scale=scales[:, t * P : (t + 1) * P],
                     rhs=v_c[a][:].bitcast(FP8X4),
                     rhs_scale=v_s[:, a, :].bitcast(U8),
-                    start=(g, a) == (1, 0),
+                    start=False,
                     stop=(a == PASSES - 1),
                 )
 
         def quantise_drift(g):
-            h_rows = late.tile([P, PACK, S], BF16, name="planes%d" % g, tag=("wl_raw10", "planes1")[g], align_bytes=ALIGN)
             half = S // 2
             if g == 0:
-                packed_v = tile([P, half, PACK], BF16, "packed_v0", "packed0")
-                h_c.append(tile([P, S], U32, "h_c0"))
+                rows = [tile([P, PACK, half], BF16, "rows0%d" % c, "rows%d" % c)[:] for c in range(2)]
+                for t in range(PACK):
+                    for c in range(2):
+                        nc.scalar.activation(
+                            rows[c][:, t, :], banks[t][:, c * half : (c + 1) * half], ACT.Abs, bias=bd_col[:, g, t : t + 1]
+                        )
+                h_c.append(late.tile([P, S], U32, name="h_c0", tag="wl_raw11", align_bytes=ALIGN))
+                pieces = [
+                    (nc.scalar.copy, tile([P, half, PACK], BF16, "packed01"), 1),
+                    (nc.vector.tensor_copy, tile([P, half, PACK], BF16, "packed00", "packed0"), 0),
+                ]
             else:
-                packed_v = shared_tile([P, half, PACK], BF16, "packed_v1", 0)
-                h_c.append(shared_tile([P, S], U32, "h_c1", WORD * S2))
-            packed_s = tile([P, half, PACK], BF16, "packed_s%d" % g)
-            for t in range(PACK):
-                nc.scalar.activation(h_rows[:, t, :], banks[g * PACK + t][:], ACT.Abs, bias=bd_col[:, g, t : t + 1])
-            nc.scalar.copy(
-                packed_s[:].rearrange("p (c i) t -> p c t i", i=RUN),
-                h_rows[:, :, half:S].rearrange("p t (c i) -> p c t i", i=RUN),
-            )
-            nc.vector.tensor_copy(
-                packed_v[:].rearrange("p (c i) t -> p c t i", i=RUN),
-                h_rows[:, :, 0:half].rearrange("p t (c i) -> p c t i", i=RUN),
-            )
-            for packed, n0 in ((packed_s, half), (packed_v, 0)):
+                h_rows = tile([P, PACK, S], BF16, "rows1", "rows1")
+                for t in range(PACK):
+                    nc.scalar.activation(h_rows[:, t, :], banks[PACK + t][:], ACT.Abs, bias=bd_col[:, g, t : t + 1])
+                rows = [h_rows[:, :, c * half : (c + 1) * half] for c in range(2)]
+                h_c.append(shared_tile([P, S], U32, "h_c1", 0))
+                pieces = [
+                    (nc.scalar.copy, shared_tile([P, half, PACK], BF16, "packed1%d" % c, 2 * WORD * T2 + c * 2 * PACK * half), c)
+                    for c in range(2)
+                ]
+            for copy, packed, c in pieces:
+                copy(
+                    packed[:].rearrange("p (c i) t -> p c t i", i=RUN),
+                    rows[c].rearrange("p t (c i) -> p c t i", i=RUN),
+                )
+            for copy, packed, c in pieces:
                 nc.vector.quantize_mx(
-                    out=h_c[g][:, n0 : n0 + half].bitcast(FP8X4),
-                    scales=h_s[g][:, n0 : n0 + half],
+                    out=h_c[g][:, c * half : (c + 1) * half].bitcast(FP8X4),
+                    scales=h_s[g][:, c * half : (c + 1) * half],
                     in_=packed[:].rearrange("p n t -> p (n t)"),
                 )
 
@@ -245,19 +273,25 @@ def tile_list_session_drift_novelty_kernel(
             )
 
         add_short_term(0, 0)
-        add_short_term(0, 1)
-        subtract_long_term(0, 0)
-        subtract_long_term(0, 1)
-        subtract_long_term(1, 0)
         add_short_term(1, 0)
-        subtract_long_term(1, 1)
+        subtract_long_term(0, 0)
+        v_c.append(head.tile([P, S], U32, name="v_c1", offset=WORD * T + S2 // 2, align_bytes=ALIGN))
+        nc.vector.tensor_copy(v_c[1][:], tab_w[1][:].bitcast(U32).indirect(idx[:]))
+        add_short_term(0, 1)
+        subtract_long_term(0, 1)
+        add_short_term(1, 1)
+        subtract_long_term(1, 0)
+        subtract_long_term(1, 1, 0, 2)
+        subtract_long_term(1, 1, 2, 2)
         quantise_drift(0)
+        nc.tensor.transpose(banks[0][:, 0:P], bc_rows[:], ident[:])
+        nc.scalar.activation(bc_col[:], banks[0][:, 0 : S2 // P], ACT.Copy)
         v2_c.append(tile([P, S2], U32, "v2_c0", "packed0"))
         gather_v2(0)
         quantise_drift(1)
         for u in range(S2 // P):
             add_scores(0, u)
-        v2_c.append(shared_tile([P, S2], U32, "v2_c1", 0))
+        v2_c.append(shared_tile([P, S2], U32, "v2_c1", 2 * WORD * T2))
         gather_v2(1)
         for u in range(S2 // P):
             add_scores(1, u)

@@ -61,10 +61,6 @@ def tile_list_session_drift_novelty_kernel(
         ident = tile([P, P], F32, "ident")
         bc_col = tile([P, S2 // P], F32, "bc_col")
         chunk0 = WORD * T + WORD * H
-        warm_in = tile([P, 8], F32, "warm_in")
-        warm = tile([P, 8], F32, "warm")
-        nc.gpsimd.memset(warm_in[:], 0.0)
-        nc.scalar.activation(warm[:], warm_in[:], ACT.Sigmoid)
         zeros = [
             head.tile([P, P // 2], F32, name="zeros0", offset=0, align_bytes=ALIGN),
             head.tile([P, P // 2], F32, name="zeros1", offset=chunk0 - P),

@@ -54,7 +54,7 @@ def tile_list_session_drift_novelty_kernel(
         ws_sraw = head.tile([P, PASSES, H // WORD], I32, name="ws_sraw", offset=WORD * T, align_bytes=ALIGN)
         ws_raw = tile([P, PASSES, 2 * H // WORD], I32, "ws_raw")
         v_s = tile([P, PASSES, S // WORD], I32, "v_s")
-        v2_s = tile([P, PASSES, S2 // WORD], I32, "v2_s")
+        v2_s = [tile([P, PASSES, GATHER // WORD], I32, "v2_s%d" % c) for c in range(S2 // GATHER)]
         tab2_s = shared_tile([P, T2 // WORD], I32, "tab2_s", WORD * T2 - T2 // 2)
         banks = [psum.tile([P, S], F32, name="bank%d" % b) for b in range(BANKS)]
 
@@ -106,7 +106,8 @@ def tile_list_session_drift_novelty_kernel(
             nc.gpsimd.memset(tab2_s[:], 0)
             half_identity(1)
             nc.vector.memset(v_s[:], 0)
-            nc.vector.memset(v2_s[:], 0)
+            for part in v2_s:
+                nc.vector.memset(part[:], 0)
             nc.sync.dma_start(ws_raw[:], ws_words.rearrange("a p c -> p a c").bitcast(I32))
             nc.sync.dma_start(idx[:], offs)
             nc.sync.dma_start(idx2[:], offs2)
@@ -154,19 +155,12 @@ def tile_list_session_drift_novelty_kernel(
         v2_g = head.tile([P, S2], U8, name="v2_g", offset=WORD * T - S2 // 2, align_bytes=ALIGN)
         nc.vector.tensor_copy(v2_g[:], tab2_s[:].bitcast(U8).indirect(idx2[:]))
 
-        def move_v2_scale_rows(a):
-            for quad in QUAD_ORDER:
-                first = QUAD * quad
-                nc.sync.dma_start(
-                    v2_s[first + V2_ROW : first + V2_ROW + ROWS, a, :],
-                    v2_g[first + 4 * a : first + QUAD : 8, :].bitcast(I32),
-                )
-
         tab2_w = [shared_tile([P, T2], I32, "tab2_w%d" % a, a * WORD * T2) for a in range(PASSES)]
-        move_v2_scale_rows(0)
         for a in range(PASSES):
             load_words(tab2_w[a], tab2_words[a])
-        move_v2_scale_rows(1)
+        for c in range(S2 // GATHER):
+            for quad in QUAD_ORDER:
+                move_scale_rows(v2_s[c], V2_ROW, v2_g[:, c * GATHER : (c + 1) * GATHER], quad)
 
         def add_short_term(g, a, slots=range(PACK)):
             for t in slots:
@@ -257,15 +251,16 @@ def tile_list_session_drift_novelty_kernel(
                     tab2_w[a][:].bitcast(U32).indirect(idx2[:, c * GATHER // 16 : (c + 1) * GATHER // 16]),
                 )
 
-        def add_scores(a, u):
+        def add_scores(a, u, start):
+            c, col = divmod(u * P, GATHER)
             nc.tensor.matmul_mx(
                 out=banks[u][:],
                 lhsT=v2_c[a][:, u * P : (u + 1) * P].bitcast(FP8X4),
-                lhsT_scale=v2_s[V2_ROW:P, a, u * P // WORD : (u + 1) * P // WORD].bitcast(U8),
+                lhsT_scale=v2_s[c][V2_ROW:P, a, col // WORD : (col + P) // WORD].bitcast(U8),
                 rhs=h_c[a][:].bitcast(FP8X4),
                 rhs_scale=h_s[a][:],
-                start=(a == 0),
-                stop=(a == PASSES - 1),
+                start=start,
+                stop=not start,
             )
 
         add_short_term(0, 0)
@@ -285,12 +280,23 @@ def tile_list_session_drift_novelty_kernel(
         v2_c.append(tile([P, S2], U32, "v2_c0", "packed0"))
         gather_v2(0)
         quantise_drift(1)
-        for u in range(S2 // P):
-            add_scores(0, u)
+        for rep in range(4):
+            nc.tensor.matmul_mx(
+                out=banks[BANKS - 1][:],
+                lhsT=v2_c[0][:, S2 - P : S2].bitcast(FP8X4),
+                lhsT_scale=h_s[0][:, 0:P],
+                rhs=h_c[0][:].bitcast(FP8X4),
+                rhs_scale=h_s[0][:],
+                start=True,
+                stop=True,
+            )
+        add_scores(0, 0, True)
         v2_c.append(shared_tile([P, S2], U32, "v2_c1", 2 * WORD * T2))
         gather_v2(1)
         for u in range(S2 // P):
-            add_scores(1, u)
+            add_scores(1, u, u > 0)
+            if u > 0:
+                add_scores(0, u, False)
             res = tile([P, S], F32, "res%d" % u)
             nc.scalar.activation(res[:], banks[u][:], ACT.Sigmoid, bias=bc_col[:, u : u + 1])
             nc.sync.dma_start(out[u * P : (u + 1) * P, :], res[:])

@@ -179,21 +179,24 @@ def tile_list_session_drift_novelty_kernel(
         h_c = []
         h_s = [tile([P, S], U8, "h_s%d" % g) for g in range(PASSES)]
 
-        def subtract_long_term(g, a, first=0, count=PACK):
-            name = "%d%d%d" % (g, a, first)
-            neg = tile([P, count, P, PACK], BF16, "neg" + name, "neg00" if (g, a) == (0, 0) else "packed0")
-            codes = tile([P, count * P], U32, "wl_c" + name)
-            if (g, a) == (0, 1):
-                scales = ws_s[ROWS:P, 3 * K_PASS : 4 * K_PASS]
-            else:
-                scales = tile([P, count * P], U8, "wl_s" + name)[:]
+        def round_wl(g, a, first, count, tag, cut):
+            neg = tile([P, count, P, PACK], BF16, "neg%d%d%d" % (g, a, first), tag)
             src = wl_raw[g, a][:].rearrange("p j (m t) -> p m j t", t=PACK)[:, :, :, first : first + count]
             dst = neg[:].rearrange("p t m j -> p m j t")
-            cut = VECTOR_COLUMNS[g, a]
             if cut < P:
                 nc.scalar.activation(dst[:, cut:P], src[:, cut:P], ACT.Copy, scale=-1.0)
             if cut:
                 nc.vector.tensor_scalar(dst[:, 0:cut], src[:, 0:cut], -1.0, None, ALU.mult)
+            return neg
+
+        def subtract_long_term(g, a, first, count, neg):
+            name = "%d%d%d" % (g, a, first)
+            codes = tile([P, count * P], U32, "wl_c" + name)
+            if (g, a) == (0, 1):
+                at = 3 * K_PASS + first * P
+                scales = ws_s[ROWS:P, at : at + count * P]
+            else:
+                scales = tile([P, count * P], U8, "wl_s" + name)[:]
             nc.vector.quantize_mx(
                 out=codes[:].bitcast(FP8X4), scales=scales, in_=neg[:].rearrange("p t m j -> p (t m j)")
             )
@@ -208,6 +211,11 @@ def tile_list_session_drift_novelty_kernel(
                     stop=(a == PASSES - 1),
                 )
 
+        def subtract_in_pairs(g, a, cuts):
+            negs = [round_wl(g, a, 2 * n, 2, "packed%d" % n, cuts[n]) for n in range(2)]
+            for n in range(2):
+                subtract_long_term(g, a, 2 * n, 2, negs[n])
+
         def quantise_drift(g):
             half = S // 2
             if g == 0:
@@ -220,7 +228,7 @@ def tile_list_session_drift_novelty_kernel(
                 h_c.append(late.tile([P, S], U32, name="h_c0", tag="wl_raw11", align_bytes=ALIGN))
                 pieces = [
                     (nc.scalar.copy, tile([P, half, PACK], BF16, "packed01"), 1),
-                    (nc.vector.tensor_copy, tile([P, half, PACK], BF16, "packed00", "packed0"), 0),
+                    (nc.vector.tensor_copy, tile([P, half, PACK], BF16, "packed00", "packed1"), 0),
                 ]
             else:
                 h_rows = tile([P, PACK, S], BF16, "rows1", "rows1")
@@ -265,19 +273,18 @@ def tile_list_session_drift_novelty_kernel(
 
         add_short_term(0, 0)
         add_short_term(1, 0)
-        subtract_long_term(0, 0)
+        subtract_long_term(0, 0, 0, PACK, round_wl(0, 0, 0, PACK, "neg00", 0))
         v_c.append(head.tile([P, S], U32, name="v_c1", offset=WORD * T + S2 // 2, align_bytes=ALIGN))
         nc.vector.tensor_copy(v_c[1][:], tab_w[1][:].bitcast(U32).indirect(idx[:]))
         add_short_term(0, 1)
-        subtract_long_term(0, 1)
+        subtract_in_pairs(0, 1, (P, 0))
         add_short_term(1, 1)
-        subtract_long_term(1, 0)
-        subtract_long_term(1, 1, 0, 2)
-        subtract_long_term(1, 1, 2, 2)
+        subtract_in_pairs(1, 0, (P, P))
+        subtract_in_pairs(1, 1, (P, P))
         quantise_drift(0)
         nc.tensor.transpose(banks[0][:, 0:P], bc_rows[:], ident[:])
         nc.scalar.activation(bc_col[:], banks[0][:, 0 : S2 // P], ACT.Copy)
-        v2_c.append(tile([P, S2], U32, "v2_c0", "packed0"))
+        v2_c.append(tile([P, S2], U32, "v2_c0", "packed1"))
         gather_v2(0)
         quantise_drift(1)
         for rep in range(4):

@@ -28,6 +28,8 @@ BANKS = 8
 V2_ROW = 4
 VECTOR_COLUMNS = {(0, 0): 0, (0, 1): 96, (1, 0): 128, (1, 1): 128}
 GATHER = 512
+SCALE_RUNS = ((0, 256), (256, 256), (512, 512))
+AHEAD = 2
 ALIGN = 256
 QUAD_ORDER = (0, 2, 1, 3)
 RUN = 4
@@ -54,7 +56,7 @@ def tile_list_session_drift_novelty_kernel(
         ws_sraw = head.tile([P, PASSES, H // WORD], I32, name="ws_sraw", offset=WORD * T, align_bytes=ALIGN)
         ws_raw = tile([P, PASSES, 2 * H // WORD], I32, "ws_raw")
         v_s = tile([P, PASSES, S // WORD], I32, "v_s")
-        v2_s = [tile([P, PASSES, GATHER // WORD], I32, "v2_s%d" % c) for c in range(S2 // GATHER)]
+        v2_s = [tile([P, PASSES, count // WORD], I32, "v2_s%d" % first) for first, count in SCALE_RUNS]
         tab2_s = shared_tile([P, T2 // WORD], I32, "tab2_s", WORD * T2 - T2 // 2)
         banks = [psum.tile([P, S], F32, name="bank%d" % b) for b in range(BANKS)]
 
@@ -158,9 +160,9 @@ def tile_list_session_drift_novelty_kernel(
         tab2_w = [shared_tile([P, T2], I32, "tab2_w%d" % a, a * WORD * T2) for a in range(PASSES)]
         for a in range(PASSES):
             load_words(tab2_w[a], tab2_words[a])
-        for c in range(S2 // GATHER):
+        for part, (first, count) in zip(v2_s, SCALE_RUNS):
             for quad in QUAD_ORDER:
-                move_scale_rows(v2_s[c], V2_ROW, v2_g[:, c * GATHER : (c + 1) * GATHER], quad)
+                move_scale_rows(part, V2_ROW, v2_g[:, first : first + count], quad)
 
         def add_short_term(g, a, slots=range(PACK)):
             for t in slots:
@@ -259,14 +261,15 @@ def tile_list_session_drift_novelty_kernel(
                     tab2_w[a][:].bitcast(U32).indirect(idx2[:, c * GATHER // 16 : (c + 1) * GATHER // 16]),
                 )
 
-        def add_scores(a, u, start):
-            c, col = divmod(u * P, GATHER)
+        def add_scores(a, u, bank, cols, start):
+            run = max(c for c, (first, count) in enumerate(SCALE_RUNS) if first <= u * P)
+            col = u * P - SCALE_RUNS[run][0]
             nc.tensor.matmul_mx(
-                out=banks[u][:],
+                out=banks[bank][:, cols],
                 lhsT=v2_c[a][:, u * P : (u + 1) * P].bitcast(FP8X4),
-                lhsT_scale=v2_s[c][V2_ROW:P, a, col // WORD : (col + P) // WORD].bitcast(U8),
-                rhs=h_c[a][:].bitcast(FP8X4),
-                rhs_scale=h_s[a][:],
+                lhsT_scale=v2_s[run][V2_ROW:P, a, col // WORD : (col + P) // WORD].bitcast(U8),
+                rhs=h_c[a][:, cols].bitcast(FP8X4),
+                rhs_scale=h_s[a][:, cols],
                 start=start,
                 stop=not start,
             )
@@ -289,7 +292,7 @@ def tile_list_session_drift_novelty_kernel(
         quantise_drift(1)
         for rep in range(4):
             nc.tensor.matmul_mx(
-                out=banks[BANKS - 1][:],
+                out=banks[BANKS - 2][:],
                 lhsT=v2_c[0][:, S2 - P : S2].bitcast(FP8X4),
                 lhsT_scale=h_s[0][:, 0:P],
                 rhs=h_c[0][:].bitcast(FP8X4),
@@ -297,13 +300,17 @@ def tile_list_session_drift_novelty_kernel(
                 start=True,
                 stop=True,
             )
-        add_scores(0, 0, True)
+        pieces = [(0, BANKS - 1, slice(0, S // 2)), (0, 0, slice(S // 2, S))]
+        pieces = pieces + [(u, u, slice(0, S)) for u in range(1, S2 // P)]
+        for u, bank, cols in pieces:
+            if u < AHEAD:
+                add_scores(0, u, bank, cols, True)
         v2_c.append(shared_tile([P, S2], U32, "v2_c1", 2 * WORD * T2))
         gather_v2(1)
-        for u in range(S2 // P):
-            add_scores(1, u, u > 0)
-            if u > 0:
-                add_scores(0, u, False)
-            res = tile([P, S], F32, "res%d" % u)
-            nc.scalar.activation(res[:], banks[u][:], ACT.Sigmoid, bias=bc_col[:, u : u + 1])
-            nc.sync.dma_start(out[u * P : (u + 1) * P, :], res[:])
+        for u, bank, cols in pieces:
+            add_scores(1, u, bank, cols, u >= AHEAD)
+            if u >= AHEAD:
+                add_scores(0, u, bank, cols, False)
+            res = tile([P, cols.stop - cols.start], F32, "res%d_%d" % (u, cols.start))
+            nc.scalar.activation(res[:], banks[bank][:, cols], ACT.Sigmoid, bias=bc_col[:, u : u + 1])
+            nc.sync.dma_start(out[u * P : (u + 1) * P, cols], res[:])

@@ -64,22 +64,10 @@ def tile_list_session_drift_novelty_kernel(
         bc_col = tile([P, S2 // P], F32, "bc_col")
         chunk0 = WORD * T + WORD * H
         zeros = [
-            head.tile([P, P // 2], F32, name="zeros0", offset=0, align_bytes=ALIGN),
-            head.tile([P, P // 2], F32, name="zeros1", offset=chunk0 - P),
+            head.tile([P, P], F32, name="zeros0", offset=0, align_bytes=ALIGN),
+            head.tile([P, P], F32, name="zeros1", offset=chunk0 - 2 * P, align_bytes=ALIGN),
         ]
-        for source in zeros:
-            nc.gpsimd.memset(source[:], 0.0)
-
-        def half_identity(c):
-            nc.gpsimd.affine_select(
-                out=ident[:, c * P // 2 : (c + 1) * P // 2],
-                in_=zeros[c][:],
-                compare_op=ALU.not_equal,
-                fill=1.0,
-                base=-c * P // 2,
-                pattern=[[-1, P // 2]],
-                channel_multiplier=1,
-            )
+        bc_rows = tile([P, P], F32, "bc_rows")
 
         wl_raw = {}
 
@@ -102,25 +90,29 @@ def tile_list_session_drift_novelty_kernel(
         ws_c = tile([P, PASSES * H * 2], U8, "ws_c")
         with tc.tile_pool(name="first", bufs=1) as first_pool:
             tab_s = first_pool.tile([P, T // WORD], I32, name="tab_s", align_bytes=ALIGN)
-            nc.gpsimd.memset(tab_s[:], 0)
-            half_identity(0)
             nc.gpsimd.memset(ws_sraw[:], 0)
-            nc.gpsimd.memset(tab2_s[:], 0)
-            half_identity(1)
+            nc.vector.memset(tab_s[:], 0)
+            nc.vector.memset(zeros[0][:], 0.0)
+            nc.vector.tensor_copy(bc_rows[:], zeros[0][:])
+            nc.vector.memset(tab2_s[:], 0)
+            nc.vector.memset(zeros[1][:], 0.0)
+            nc.gpsimd.affine_select(
+                out=ident[:], in_=zeros[1][:], compare_op=ALU.not_equal, fill=1.0, base=0, pattern=[[-1, P]], channel_multiplier=1
+            )
             nc.vector.memset(v_s[:], 0)
             for part in v2_s:
                 nc.vector.memset(part[:], 0)
-            nc.sync.dma_start(ws_raw[:], ws_words.rearrange("a p c -> p a c").bitcast(I32))
             nc.sync.dma_start(idx[:], offs)
+            nc.sync.dma_start(ws_raw[:], ws_words.rearrange("a p c -> p a c").bitcast(I32))
             nc.sync.dma_start(idx2[:], offs2)
-            load_scale_table(tab_s, tab_scales)
-            tab_w = [head.tile([P, T], I32, name="tab_w0", offset=0, align_bytes=ALIGN)]
-            load_words(tab_w[0], tab_words[0])
             for s in range(ROWS):
                 nc.sync.dma_start(
                     ws_sraw[s:P:QUAD, :, :],
                     ws_scales[:, s : QUADS * ROWS : ROWS, :].rearrange("a q c -> q a c").bitcast(I32),
                 )
+            load_scale_table(tab_s, tab_scales)
+            tab_w = [head.tile([P, T], I32, name="tab_w0", offset=0, align_bytes=ALIGN)]
+            load_words(tab_w[0], tab_words[0])
             load_scale_table(tab2_s, tab2_scales)
             wl_raw.setdefault((0, 0), head.tile([P, PACK, K_PASS], F32, name="wl_raw00", offset=chunk0, align_bytes=ALIGN))
             load_wl(0, 0)
@@ -140,8 +132,6 @@ def tile_list_session_drift_novelty_kernel(
             move_scale_rows(v_s, 0, v_g, quad)
         tab_w.append(late.tile([P, T], I32, name="tab_w1", align_bytes=ALIGN))
         load_words(tab_w[1], tab_words[1])
-        bc_rows = late.tile([P, P], F32, name="bc_rows", align_bytes=ALIGN)
-        nc.gpsimd.memset(bc_rows[:], 0.0)
         bd_col = late.tile([P, PASSES, 2 * PACK], F32, name="bd_col", align_bytes=ALIGN)
         for g, a in late_chunks:
             load_wl(g, a)

@@ -1,6 +1,7 @@
 from contextlib import ExitStack
 
 import concourse.mybir as mybir
+from concourse.masks import make_identity
 
 K, H, T, S, T2, S2 = 1024, 1024, 2048, 512, 4096, 1024
 FLOPS = 2 * (2 * K * H * S + H * S2 * S)
@@ -25,14 +26,16 @@ QUAD = P // QUADS
 ROWS = 4
 WORD = 4
 BANKS = 8
+KIB = 1024
 V2_ROW = 4
-VECTOR_COLUMNS = {(0, 0): 0, (0, 1): 96, (1, 0): 128, (1, 1): 128}
-GATHER = 512
-SCALE_RUNS = ((0, 256), (256, 256), (512, 512))
-AHEAD = 2
+TABLE_FIRST, TABLE_STEP = 32, 2
+BC_FIRST, BC_STEP = 36, 4
+GATHERS = (((0, 512), (512, 512)), ((0, 256), (256, 256), (512, 512)))
+SCALE_RUNS = ((0, 256), (256, 768))
 ALIGN = 256
 QUAD_ORDER = (0, 2, 1, 3)
 RUN = 4
+WARM_UPS = 4
 
 
 def tile_list_session_drift_novelty_kernel(
@@ -41,124 +44,115 @@ def tile_list_session_drift_novelty_kernel(
     nc = tc.nc
     with ExitStack() as ctx:
         keep = ctx.enter_context(tc.tile_pool(name="keep", bufs=1))
-        shared = ctx.enter_context(tc.tile_pool(name="shared", bufs=1))
+        placed = ctx.enter_context(tc.tile_pool(name="placed", bufs=1))
         psum = ctx.enter_context(tc.psum_pool(name="psum", bufs=1))
 
-        def tile(shape, dtype, name, tag=""):
-            return keep.tile(shape, dtype, name=name, tag=tag, align_bytes=ALIGN)
+        def tile(shape, dtype, name):
+            return keep.tile(shape, dtype, name=name, align_bytes=ALIGN)
 
-        def shared_tile(shape, dtype, name, offset):
-            return shared.tile(shape, dtype, name=name, offset=offset, align_bytes=ALIGN)
+        def place(shape, dtype, name, offset):
+            return placed.tile(shape, dtype, name=name, offset=offset, align_bytes=ALIGN)
+
+        at_v2 = 0
+        at_v = at_v2 + PASSES * WORD * T2
+        at_pairs = at_v + PASSES * WORD * T
+        at_late = at_pairs + 4 * KIB
 
         idx = keep.tile([P, S // 16], U16, name="idx")
         idx2 = keep.tile([P, S2 // 16], U16, name="idx2")
-        head = ctx.enter_context(tc.tile_pool(name="head", bufs=1))
-        ws_sraw = head.tile([P, PASSES, H // WORD], I32, name="ws_sraw", offset=WORD * T, align_bytes=ALIGN)
+        banks = [psum.tile([P, S], F32, name="bank%d" % b) for b in range(BANKS)]
         ws_raw = tile([P, PASSES, 2 * H // WORD], I32, "ws_raw")
+        ws_sraw = tile([P, PASSES, H // WORD], I32, "ws_sraw")
+        ws_c = tile([P, PASSES * H * 2], U8, "ws_c")
+        ws_s = tile([P, PASSES * H], U8, "ws_s")
+        tab2_s = place([P, T2 // WORD], I32, "tab2_s", at_v2 + WORD * T2 - T2 // 2)
+        zeros = place([P, P], F32, "zeros", at_v)
+        bc_rows = tile([P, P], F32, "bc_rows")
+        bc_col = tile([P, S2 // P], F32, "bc_col")
+        ident = tile([P, P], F32, "ident")
         v_s = tile([P, PASSES, S // WORD], I32, "v_s")
         v2_s = [tile([P, PASSES, count // WORD], I32, "v2_s%d" % first) for first, count in SCALE_RUNS]
-        tab2_s = shared_tile([P, T2 // WORD], I32, "tab2_s", WORD * T2 - T2 // 2)
-        banks = [psum.tile([P, S], F32, name="bank%d" % b) for b in range(BANKS)]
-
-        ident = tile([P, P], F32, "ident")
-        bc_col = tile([P, S2 // P], F32, "bc_col")
-        chunk0 = WORD * T + WORD * H
-        zeros = [
-            head.tile([P, P], F32, name="zeros0", offset=0, align_bytes=ALIGN),
-            head.tile([P, P], F32, name="zeros1", offset=chunk0 - 2 * P, align_bytes=ALIGN),
-        ]
-        bc_rows = tile([P, P], F32, "bc_rows")
-
-        wl_raw = {}
+        v_g = tile([P, S], U8, "v_g")
+        v2_g = tile([P, S2], U8, "v2_g")
 
         def load_scale_table(dst, src):
-            nc.sync.dma_start(dst[0:P:4, :], src.rearrange("a q c -> q a c").bitcast(I32))
+            rows = slice(TABLE_FIRST, TABLE_FIRST + TABLE_STEP * PASSES * QUADS * ROWS, TABLE_STEP)
+            nc.sync.dma_start(dst[rows, :], src.rearrange("a q c -> q a c").bitcast(I32))
 
         def move_scale_rows(dst, row, src, quad):
-            first = QUAD * quad
-            nc.sync.dma_start(dst[first + row : first + row + ROWS, :, :], src[first : first + QUAD : 4, :].bitcast(I32))
-
-        def load_words(dst, src):
-            nc.sync.dma_start(dst[:], src.rearrange("p t i -> p (t i)").bitcast(I32))
-
-        def load_wl(g, a):
+            span = TABLE_STEP * PASSES * ROWS
+            first = TABLE_FIRST + span * quad
             nc.sync.dma_start(
-                wl_raw[g, a][:],
-                wl[a * K_PASS : (a + 1) * K_PASS, g * K_PASS : (g + 1) * K_PASS].rearrange("(p j) c -> p j c", j=PACK),
+                dst[QUAD * quad + row : QUAD * quad + row + ROWS, :, :],
+                src[first : first + span : TABLE_STEP, :].bitcast(I32),
             )
 
-        ws_c = tile([P, PASSES * H * 2], U8, "ws_c")
         with tc.tile_pool(name="first", bufs=1) as first_pool:
             tab_s = first_pool.tile([P, T // WORD], I32, name="tab_s", align_bytes=ALIGN)
             nc.gpsimd.memset(ws_sraw[:], 0)
             nc.vector.memset(tab_s[:], 0)
-            nc.vector.memset(zeros[0][:], 0.0)
-            nc.vector.tensor_copy(bc_rows[:], zeros[0][:])
             nc.vector.memset(tab2_s[:], 0)
-            nc.vector.memset(zeros[1][:], 0.0)
-            nc.gpsimd.affine_select(
-                out=ident[:], in_=zeros[1][:], compare_op=ALU.not_equal, fill=1.0, base=0, pattern=[[-1, P]], channel_multiplier=1
-            )
+            nc.vector.memset(zeros[:], 0.0)
+            nc.vector.tensor_copy(bc_rows[:], zeros[:])
             nc.vector.memset(v_s[:], 0)
             for part in v2_s:
                 nc.vector.memset(part[:], 0)
+            make_identity(nc, ident[:])
             nc.sync.dma_start(idx[:], offs)
-            nc.sync.dma_start(ws_raw[:], ws_words.rearrange("a p c -> p a c").bitcast(I32))
             nc.sync.dma_start(idx2[:], offs2)
+            nc.sync.dma_start(ws_raw[:], ws_words.rearrange("a p c -> p a c").bitcast(I32))
+            load_scale_table(tab_s, tab_scales)
             for s in range(ROWS):
                 nc.sync.dma_start(
                     ws_sraw[s:P:QUAD, :, :],
                     ws_scales[:, s : QUADS * ROWS : ROWS, :].rearrange("a q c -> q a c").bitcast(I32),
                 )
-            load_scale_table(tab_s, tab_scales)
-            tab_w = [head.tile([P, T], I32, name="tab_w0", offset=0, align_bytes=ALIGN)]
-            load_words(tab_w[0], tab_words[0])
             load_scale_table(tab2_s, tab2_scales)
-            wl_raw.setdefault((0, 0), head.tile([P, PACK, K_PASS], F32, name="wl_raw00", offset=chunk0, align_bytes=ALIGN))
-            load_wl(0, 0)
+            tab_w = place([P, PASSES, T], I32, "tab_w", at_v)
+            nc.sync.dma_start(tab_w[:], tab_words.rearrange("a p t i -> p a (t i)").bitcast(I32))
+            bc_at = slice(BC_FIRST, BC_FIRST + BC_STEP * (S2 // P), BC_STEP)
+            nc.sync.dma_start(bc_rows[bc_at, :], bc.rearrange("(u m) -> u m", m=P))
             nc.vector.tensor_copy(
                 ws_c[:].bitcast(U16).rearrange("p (b t m) -> p b t m", t=PACK, m=P),
                 ws_raw[:].rearrange("p a c -> p (a c)").bitcast(U16).rearrange("p (b m t) -> p b t m", t=PACK, m=P),
             )
-            v_g = head.tile([P, S], U8, name="v_g", offset=chunk0 - S, align_bytes=ALIGN)
             nc.vector.tensor_copy(v_g[:], tab_s[:].bitcast(U8).indirect(idx[:]))
         late = ctx.enter_context(tc.tile_pool(name="late", bufs=1))
-        ws_s = late.tile([P, PASSES * H], U8, name="ws_s", align_bytes=ALIGN)
-        late_chunks = ((0, 1), (1, 0), (1, 1))
-        for g, a in late_chunks:
-            name = "wl_raw%d%d" % (g, a)
-            wl_raw.setdefault((g, a), late.tile([P, PACK, K_PASS], F32, name=name, tag=name, align_bytes=ALIGN))
         for quad in QUAD_ORDER:
             move_scale_rows(v_s, 0, v_g, quad)
-        tab_w.append(late.tile([P, T], I32, name="tab_w1", align_bytes=ALIGN))
-        load_words(tab_w[1], tab_words[1])
+        wl_rows = wl.rearrange("(a p j) c -> a p j c", a=PASSES, j=PACK)
+        wl_first = late.tile([P, PACK, H], F32, name="wl_first", align_bytes=ALIGN)
+        nc.sync.dma_start(wl_first[:], wl_rows[0])
         bd_col = late.tile([P, PASSES, 2 * PACK], F32, name="bd_col", align_bytes=ALIGN)
-        for g, a in late_chunks:
-            load_wl(g, a)
-            if (g, a) == (0, 1):
-                nc.sync.dma_start(bd_col[:, :, 0:PACK], bd.rearrange("(g p t) -> p g t", g=PASSES, t=PACK))
-                nc.sync.dma_start(bc_rows[0 : S2 // P, :], bc.rearrange("(u m) -> u m", m=P))
-        v_c = [tile([P, S], U32, "v_c0")]
-        nc.vector.tensor_copy(v_c[0][:], tab_w[0][:].bitcast(U32).indirect(idx[:]))
+        nc.sync.dma_start(bd_col[:, :, 0:PACK], bd.rearrange("(g p t) -> p g t", g=PASSES, t=PACK))
+        wl_second = []
+        for g in range(PASSES):
+            wl_second.append(late.tile([P, PACK, K_PASS], F32, name="wl_second%d" % g, tag="second%d" % g, align_bytes=ALIGN))
+            nc.sync.dma_start(wl_second[g][:], wl_rows[1][:, :, g * K_PASS : (g + 1) * K_PASS])
+
         nc.vector.tensor_copy(
             ws_s[:].rearrange("p (b t m) -> p b t m", t=PACK, m=P),
             ws_sraw[:].rearrange("p a c -> p (a c)").bitcast(U8).rearrange("p (b m t) -> p b t m", t=PACK, m=P),
         )
-        v2_g = head.tile([P, S2], U8, name="v2_g", offset=WORD * T - S2 // 2, align_bytes=ALIGN)
         nc.vector.tensor_copy(v2_g[:], tab2_s[:].bitcast(U8).indirect(idx2[:]))
-
-        tab2_w = [shared_tile([P, T2], I32, "tab2_w%d" % a, a * WORD * T2) for a in range(PASSES)]
+        tab2_w = [place([P, T2], I32, "tab2_w%d" % a, at_v2 + a * WORD * T2) for a in range(PASSES)]
+        moves = [(part, first, count, quad) for part, (first, count) in zip(v2_s, SCALE_RUNS) for quad in QUAD_ORDER]
         for a in range(PASSES):
-            load_words(tab2_w[a], tab2_words[a])
-        for part, (first, count) in zip(v2_s, SCALE_RUNS):
-            for quad in QUAD_ORDER:
+            nc.sync.dma_start(tab2_w[a][:], tab2_words[a].rearrange("p t i -> p (t i)").bitcast(I32))
+            for part, first, count, quad in moves[0:1] if a == 0 else moves[1:]:
                 move_scale_rows(part, V2_ROW, v2_g[:, first : first + count], quad)
 
-        def add_short_term(g, a, slots=range(PACK)):
-            for t in slots:
-                col = ((a * 2 + g) * PACK + t) * P
+        nc.tensor.transpose(banks[BANKS - 1][:, 0:P], bc_rows[:], ident[:])
+        nc.scalar.activation(bc_col[:], banks[BANKS - 1][:, bc_at], ACT.Copy)
+
+        v_c = [tile([P, S], U32, "v_c%d" % a) for a in range(PASSES)]
+        for a in range(PASSES):
+            nc.vector.tensor_copy(v_c[a][:], tab_w[:, a, :].bitcast(U32).indirect(idx[:]))
+        for a in range(PASSES):
+            for b in range(BANKS):
+                col = (a * BANKS + b) * P
                 nc.tensor.matmul_mx(
-                    out=banks[g * PACK + t][:],
+                    out=banks[b][:],
                     lhsT=ws_c[:, 2 * col : 2 * col + 2 * P].bitcast(FP4X4),
                     lhsT_scale=ws_s[:, col : col + P],
                     rhs=v_c[a][:].bitcast(FP8X4),
@@ -167,30 +161,19 @@ def tile_list_session_drift_novelty_kernel(
                     stop=False,
                 )
 
-        v2_c = []
-        h_c = []
-        h_s = [tile([P, S], U8, "h_s%d" % g) for g in range(PASSES)]
-
-        def round_wl(g, a, first, count, tag, cut):
-            neg = tile([P, count, P, PACK], BF16, "neg%d%d%d" % (g, a, first), tag)
-            src = wl_raw[g, a][:].rearrange("p j (m t) -> p m j t", t=PACK)[:, :, :, first : first + count]
-            dst = neg[:].rearrange("p t m j -> p m j t")
-            if cut < P:
-                nc.scalar.activation(dst[:, cut:P], src[:, cut:P], ACT.Copy, scale=-1.0)
-            if cut:
-                nc.vector.tensor_scalar(dst[:, 0:cut], src[:, 0:cut], -1.0, None, ALU.mult)
-            return neg
+        def wl_view(g, a, first, count):
+            rows = wl_first[:, :, g * K_PASS : (g + 1) * K_PASS] if a == 0 else wl_second[g][:]
+            return rows.rearrange("p j (m t) -> p m j t", t=PACK)[:, :, :, first : first + count]
 
         def subtract_long_term(g, a, first, count, neg):
             name = "%d%d%d" % (g, a, first)
-            codes = tile([P, count * P], U32, "wl_c" + name)
-            if (g, a) == (0, 1):
-                at = 3 * K_PASS + first * P
-                scales = ws_s[ROWS:P, at : at + count * P]
+            if count == PACK:
+                codes = late.tile([P, count * P], U32, name="wl_c" + name, tag="second0", align_bytes=ALIGN)
             else:
-                scales = tile([P, count * P], U8, "wl_s" + name)[:]
+                codes = tile([P, count * P], U32, "wl_c" + name)
+            scales = tile([P, count * P], U8, "wl_s" + name)
             nc.vector.quantize_mx(
-                out=codes[:].bitcast(FP8X4), scales=scales, in_=neg[:].rearrange("p t m j -> p (t m j)")
+                out=codes[:].bitcast(FP8X4), scales=scales[:], in_=neg[:].rearrange("p t m j -> p (t m j)")
             )
             for t in range(count):
                 nc.tensor.matmul_mx(
@@ -203,104 +186,94 @@ def tile_list_session_drift_novelty_kernel(
                     stop=(a == PASSES - 1),
                 )
 
-        def subtract_in_pairs(g, a, cuts):
-            negs = [round_wl(g, a, 2 * n, 2, "packed%d" % n, cuts[n]) for n in range(2)]
+        def subtract_in_pairs(g, a):
+            negs = []
+            for n in range(2):
+                negs.append(place([P, 2, P, PACK], BF16, "neg%d%d%d" % (g, a, n), at_pairs + n * 2 * KIB))
+                nc.vector.tensor_scalar(
+                    negs[n][:].rearrange("p t m j -> p m j t"), wl_view(g, a, 2 * n, 2), -1.0, None, ALU.mult
+                )
             for n in range(2):
                 subtract_long_term(g, a, 2 * n, 2, negs[n])
 
-        def quantise_drift(g):
-            half = S // 2
-            if g == 0:
-                rows = [tile([P, PACK, half], BF16, "rows0%d" % c, "rows%d" % c)[:] for c in range(2)]
-                for t in range(PACK):
-                    for c in range(2):
-                        nc.scalar.activation(
-                            rows[c][:, t, :], banks[t][:, c * half : (c + 1) * half], ACT.Abs, bias=bd_col[:, g, t : t + 1]
-                        )
-                h_c.append(late.tile([P, S], U32, name="h_c0", tag="wl_raw11", align_bytes=ALIGN))
-                pieces = [
-                    (nc.scalar.copy, tile([P, half, PACK], BF16, "packed01"), 1),
-                    (nc.vector.tensor_copy, tile([P, half, PACK], BF16, "packed00", "packed1"), 0),
-                ]
-            else:
-                h_rows = tile([P, PACK, S], BF16, "rows1", "rows1")
-                for t in range(PACK):
-                    nc.scalar.activation(h_rows[:, t, :], banks[PACK + t][:], ACT.Abs, bias=bd_col[:, g, t : t + 1])
-                rows = [h_rows[:, :, c * half : (c + 1) * half] for c in range(2)]
-                h_c.append(shared_tile([P, S], U32, "h_c1", 0))
-                pieces = [
-                    (nc.scalar.copy, shared_tile([P, half, PACK], BF16, "packed1%d" % c, 2 * WORD * T2 + c * 2 * PACK * half), c)
-                    for c in range(2)
-                ]
-            for copy, packed, c in pieces:
-                copy(
-                    packed[:].rearrange("p (c i) t -> p c t i", i=RUN),
-                    rows[c].rearrange("p t (c i) -> p c t i", i=RUN),
-                )
-            for copy, packed, c in pieces:
-                nc.vector.quantize_mx(
-                    out=h_c[g][:, c * half : (c + 1) * half].bitcast(FP8X4),
-                    scales=h_s[g][:, c * half : (c + 1) * half],
-                    in_=packed[:].rearrange("p n t -> p (n t)"),
-                )
+        neg_scalar = tile([P, PACK, P, PACK], BF16, "neg10")
+        nc.scalar.activation(
+            neg_scalar[:].rearrange("p t m j -> p m j t"), wl_view(1, 0, 0, PACK), ACT.Copy, scale=-1.0
+        )
+        subtract_in_pairs(0, 0)
+        subtract_in_pairs(0, 1)
+        subtract_long_term(1, 0, 0, PACK, neg_scalar)
+        subtract_in_pairs(1, 1)
 
-        def gather_v2(a):
-            for c in range(S2 // GATHER):
-                nc.vector.tensor_copy(
-                    v2_c[a][:, c * GATHER : (c + 1) * GATHER],
-                    tab2_w[a][:].bitcast(U32).indirect(idx2[:, c * GATHER // 16 : (c + 1) * GATHER // 16]),
-                )
+        h_rows = [tile([P, PACK, S], BF16, "h_rows%d" % g) for g in range(PASSES)]
+        h_c = [tile([P, S], U32, "h_c0")]
+        h_s = [tile([P, S], U8, "h_s%d" % g) for g in range(PASSES)]
+        for g in range(PASSES):
+            for t in range(PACK):
+                nc.scalar.activation(h_rows[g][:, t, :], banks[g * PACK + t][:], ACT.Abs, bias=bd_col[:, g, t : t + 1])
 
-        def add_scores(a, u, bank, cols, start):
-            run = max(c for c, (first, count) in enumerate(SCALE_RUNS) if first <= u * P)
-            col = u * P - SCALE_RUNS[run][0]
-            nc.tensor.matmul_mx(
-                out=banks[bank][:, cols],
-                lhsT=v2_c[a][:, u * P : (u + 1) * P].bitcast(FP8X4),
-                lhsT_scale=v2_s[run][V2_ROW:P, a, col // WORD : (col + P) // WORD].bitcast(U8),
-                rhs=h_c[a][:, cols].bitcast(FP8X4),
-                rhs_scale=h_s[a][:, cols],
-                start=start,
-                stop=not start,
+        def interleave(copy, packed, g, cols):
+            copy(
+                packed[:, cols, :].rearrange("p (c i) t -> p c t i", i=RUN),
+                h_rows[g][:, :, cols].rearrange("p t (c i) -> p c t i", i=RUN),
             )
 
-        add_short_term(0, 0)
-        add_short_term(1, 0)
-        subtract_long_term(0, 0, 0, PACK, round_wl(0, 0, 0, PACK, "neg00", 0))
-        v_c.append(head.tile([P, S], U32, name="v_c1", offset=WORD * T + S2 // 2, align_bytes=ALIGN))
-        nc.vector.tensor_copy(v_c[1][:], tab_w[1][:].bitcast(U32).indirect(idx[:]))
-        add_short_term(0, 1)
-        subtract_in_pairs(0, 1, (P, 0))
-        add_short_term(1, 1)
-        subtract_in_pairs(1, 0, (P, P))
-        subtract_in_pairs(1, 1, (P, P))
-        quantise_drift(0)
-        nc.tensor.transpose(banks[0][:, 0:P], bc_rows[:], ident[:])
-        nc.scalar.activation(bc_col[:], banks[0][:, 0 : S2 // P], ACT.Copy)
-        v2_c.append(tile([P, S2], U32, "v2_c0", "packed1"))
-        gather_v2(0)
-        quantise_drift(1)
-        for rep in range(4):
+        def quantise_drift(packed, g, cols):
+            nc.vector.quantize_mx(
+                out=h_c[g][:, cols].bitcast(FP8X4),
+                scales=h_s[g][:, cols],
+                in_=packed[:, cols, :].rearrange("p n t -> p (n t)"),
+            )
+
+        halves = (slice(0, S // 2), slice(S // 2, S))
+
+        def gather_v2(words, a):
+            for first, count in GATHERS[a]:
+                nc.vector.tensor_copy(
+                    words[:, first : first + count],
+                    tab2_w[a][:].bitcast(U32).indirect(idx2[:, first // 16 : (first + count) // 16]),
+                )
+
+        packed0 = place([P, S, PACK], BF16, "packed0", at_pairs)
+        for cols in halves:
+            interleave(nc.vector.tensor_copy, packed0, 0, cols)
+        for cols in halves:
+            quantise_drift(packed0, 0, cols)
+        v2_first = place([P, S2], U32, "v2_first", at_pairs)
+        gather_v2(v2_first, 0)
+        h_c.append(place([P, S], U32, "h_c1", at_v2))
+        packed1 = place([P, S, PACK], BF16, "packed1", at_late)
+        for cols in halves:
+            interleave(nc.scalar.copy, packed1, 1, cols)
+        for cols in halves:
+            quantise_drift(packed1, 1, cols)
+        for rep in range(WARM_UPS):
             nc.tensor.matmul_mx(
-                out=banks[BANKS - 2][:],
-                lhsT=v2_c[0][:, S2 - P : S2].bitcast(FP8X4),
+                out=banks[0][:],
+                lhsT=v2_first[:, 0:P].bitcast(FP8X4),
                 lhsT_scale=h_s[0][:, 0:P],
                 rhs=h_c[0][:].bitcast(FP8X4),
                 rhs_scale=h_s[0][:],
                 start=True,
                 stop=True,
             )
-        pieces = [(0, BANKS - 1, slice(0, S // 2)), (0, 0, slice(S // 2, S))]
-        pieces = pieces + [(u, u, slice(0, S)) for u in range(1, S2 // P)]
-        for u, bank, cols in pieces:
-            if u < AHEAD:
-                add_scores(0, u, bank, cols, True)
-        v2_c.append(shared_tile([P, S2], U32, "v2_c1", 2 * WORD * T2))
-        gather_v2(1)
-        for u, bank, cols in pieces:
-            add_scores(1, u, bank, cols, u >= AHEAD)
-            if u >= AHEAD:
-                add_scores(0, u, bank, cols, False)
-            res = tile([P, cols.stop - cols.start], F32, "res%d_%d" % (u, cols.start))
-            nc.scalar.activation(res[:], banks[bank][:, cols], ACT.Sigmoid, bias=bc_col[:, u : u + 1])
-            nc.sync.dma_start(out[u * P : (u + 1) * P, cols], res[:])
+        v2_c = [v2_first, place([P, S2], U32, "v2_last", at_late)]
+        gather_v2(v2_c[1], 1)
+
+        for u in range(S2 // P):
+            run = max(c for c, (first, count) in enumerate(SCALE_RUNS) if first <= u * P)
+            col = u * P - SCALE_RUNS[run][0]
+            order = (0, 1) if u == 0 else (1, 0)
+            for a in order:
+                nc.tensor.matmul_mx(
+                    out=banks[u][:],
+                    lhsT=v2_c[a][:, u * P : (u + 1) * P].bitcast(FP8X4),
+                    lhsT_scale=v2_s[run][V2_ROW:P, a, col // WORD : (col + P) // WORD].bitcast(U8),
+                    rhs=h_c[a][:].bitcast(FP8X4),
+                    rhs_scale=h_s[a][:],
+                    start=(a == order[0]),
+                    stop=(a == order[1]),
+                )
+            res = tile([P, S], F32, "res%d" % u)
+            nc.scalar.activation(res[:], banks[u][:], ACT.Sigmoid, bias=bc_col[:, u : u + 1])
+            nc.sync.dma_start(out[u * P : (u + 1) * P, :], res[:])

@@ -1,7 +1,6 @@
 from contextlib import ExitStack
 
 import concourse.mybir as mybir
-from concourse.masks import make_identity
 
 K, H, T, S, T2, S2 = 1024, 1024, 2048, 512, 4096, 1024
 FLOPS = 2 * (2 * K * H * S + H * S2 * S)
@@ -29,7 +28,9 @@ BANKS = 8
 KIB = 1024
 V2_ROW = 4
 TABLE_FIRST, TABLE_STEP = 32, 2
-BC_FIRST, BC_STEP = 36, 4
+BC_STEP = QUAD // (S2 // P)
+BD_STEP = QUAD // PASSES
+BIAS_ROW = 1
 GATHERS = (((0, 512), (512, 512)), ((0, 256), (256, 256), (512, 512)))
 SCALE_RUNS = ((0, 256), (256, 768))
 ALIGN = 256
@@ -63,13 +64,13 @@ def tile_list_session_drift_novelty_kernel(
         banks = [psum.tile([P, S], F32, name="bank%d" % b) for b in range(BANKS)]
         ws_raw = tile([P, PASSES, 2 * H // WORD], I32, "ws_raw")
         ws_sraw = tile([P, PASSES, H // WORD], I32, "ws_sraw")
-        ws_c = tile([P, PASSES * H * 2], U8, "ws_c")
-        ws_s = tile([P, PASSES * H], U8, "ws_s")
+        ws_c = [tile([P, PASSES * K_PASS * 2], U8, "ws_c0")]
+        ws_s = [tile([P, PASSES * K_PASS], U8, "ws_s0")]
         tab2_s = place([P, T2 // WORD], I32, "tab2_s", at_v2 + WORD * T2 - T2 // 2)
         zeros = place([P, P], F32, "zeros", at_v)
-        bc_rows = tile([P, P], F32, "bc_rows")
-        bc_col = tile([P, S2 // P], F32, "bc_col")
-        ident = tile([P, P], F32, "ident")
+        bc_rows = tile([P, QUAD], F32, "bc_rows")
+        bd_rows = tile([P, P], F32, "bd_rows")
+        bd_planes = tile([P, P], F32, "bd_planes")
         v_s = tile([P, PASSES, S // WORD], I32, "v_s")
         v2_s = [tile([P, PASSES, count // WORD], I32, "v2_s%d" % first) for first, count in SCALE_RUNS]
         v_g = tile([P, S], U8, "v_g")
@@ -87,17 +88,24 @@ def tile_list_session_drift_novelty_kernel(
                 src[first : first + span : TABLE_STEP, :].bitcast(I32),
             )
 
+        def order_columns(dst, src, g, dtype):
+            columns = src[:].rearrange("p a c -> p (a c)").bitcast(dtype)
+            nc.vector.tensor_copy(
+                dst[:].bitcast(dtype).rearrange("p (a t m) -> p a t m", t=PACK, m=P),
+                columns.rearrange("p (a g m t) -> p g a t m", g=PASSES, t=PACK, m=P)[:, g],
+            )
+
         with tc.tile_pool(name="first", bufs=1) as first_pool:
             tab_s = first_pool.tile([P, T // WORD], I32, name="tab_s", align_bytes=ALIGN)
             nc.gpsimd.memset(ws_sraw[:], 0)
             nc.vector.memset(tab_s[:], 0)
             nc.vector.memset(tab2_s[:], 0)
             nc.vector.memset(zeros[:], 0.0)
-            nc.vector.tensor_copy(bc_rows[:], zeros[:])
+            nc.vector.tensor_copy(bd_rows[:], zeros[:])
+            nc.vector.memset(bc_rows[:], 0.0)
             nc.vector.memset(v_s[:], 0)
             for part in v2_s:
                 nc.vector.memset(part[:], 0)
-            make_identity(nc, ident[:])
             nc.sync.dma_start(idx[:], offs)
             nc.sync.dma_start(idx2[:], offs2)
             nc.sync.dma_start(ws_raw[:], ws_words.rearrange("a p c -> p a c").bitcast(I32))
@@ -110,12 +118,9 @@ def tile_list_session_drift_novelty_kernel(
             load_scale_table(tab2_s, tab2_scales)
             tab_w = place([P, PASSES, T], I32, "tab_w", at_v)
             nc.sync.dma_start(tab_w[:], tab_words.rearrange("a p t i -> p a (t i)").bitcast(I32))
-            bc_at = slice(BC_FIRST, BC_FIRST + BC_STEP * (S2 // P), BC_STEP)
-            nc.sync.dma_start(bc_rows[bc_at, :], bc.rearrange("(u m) -> u m", m=P))
-            nc.vector.tensor_copy(
-                ws_c[:].bitcast(U16).rearrange("p (b t m) -> p b t m", t=PACK, m=P),
-                ws_raw[:].rearrange("p a c -> p (a c)").bitcast(U16).rearrange("p (b m t) -> p b t m", t=PACK, m=P),
-            )
+            nc.sync.dma_start(bd_rows[BIAS_ROW:P:BD_STEP, :], bd.rearrange("(g h c) -> h g c", g=PASSES, h=QUADS))
+            nc.sync.dma_start(bc_rows[BIAS_ROW:P:BC_STEP, :], bc.rearrange("(u h m) -> h u m", h=QUADS, m=QUAD))
+            order_columns(ws_c[0], ws_raw, 0, U16)
             nc.vector.tensor_copy(v_g[:], tab_s[:].bitcast(U8).indirect(idx[:]))
         late = ctx.enter_context(tc.tile_pool(name="late", bufs=1))
         for quad in QUAD_ORDER:
@@ -123,17 +128,14 @@ def tile_list_session_drift_novelty_kernel(
         wl_rows = wl.rearrange("(a p j) c -> a p j c", a=PASSES, j=PACK)
         wl_first = late.tile([P, PACK, H], F32, name="wl_first", align_bytes=ALIGN)
         nc.sync.dma_start(wl_first[:], wl_rows[0])
-        bd_col = late.tile([P, PASSES, 2 * PACK], F32, name="bd_col", align_bytes=ALIGN)
-        nc.sync.dma_start(bd_col[:, :, 0:PACK], bd.rearrange("(g p t) -> p g t", g=PASSES, t=PACK))
         wl_second = []
         for g in range(PASSES):
             wl_second.append(late.tile([P, PACK, K_PASS], F32, name="wl_second%d" % g, tag="second%d" % g, align_bytes=ALIGN))
             nc.sync.dma_start(wl_second[g][:], wl_rows[1][:, :, g * K_PASS : (g + 1) * K_PASS])
 
-        nc.vector.tensor_copy(
-            ws_s[:].rearrange("p (b t m) -> p b t m", t=PACK, m=P),
-            ws_sraw[:].rearrange("p a c -> p (a c)").bitcast(U8).rearrange("p (b m t) -> p b t m", t=PACK, m=P),
-        )
+        order_columns(ws_s[0], ws_sraw, 0, U8)
+        ws_c.append(late.tile([P, PASSES * K_PASS * 2], U8, name="ws_c1", align_bytes=ALIGN))
+        order_columns(ws_c[1], ws_raw, 1, U16)
         nc.vector.tensor_copy(v2_g[:], tab2_s[:].bitcast(U8).indirect(idx2[:]))
         tab2_w = [place([P, T2], I32, "tab2_w%d" % a, at_v2 + a * WORD * T2) for a in range(PASSES)]
         moves = [(part, first, count, quad) for part, (first, count) in zip(v2_s, SCALE_RUNS) for quad in QUAD_ORDER]
@@ -142,24 +144,36 @@ def tile_list_session_drift_novelty_kernel(
             for part, first, count, quad in moves[0:1] if a == 0 else moves[1:]:
                 move_scale_rows(part, V2_ROW, v2_g[:, first : first + count], quad)
 
-        nc.tensor.transpose(banks[BANKS - 1][:, 0:P], bc_rows[:], ident[:])
-        nc.scalar.activation(bc_col[:], banks[BANKS - 1][:, bc_at], ACT.Copy)
+        nc.scalar.activation(
+            bd_planes[:].rearrange("p (t m) -> p t m", t=PACK), bd_rows[:].rearrange("p (m t) -> p t m", t=PACK), ACT.Copy
+        )
 
         v_c = [tile([P, S], U32, "v_c%d" % a) for a in range(PASSES)]
         for a in range(PASSES):
             nc.vector.tensor_copy(v_c[a][:], tab_w[:, a, :].bitcast(U32).indirect(idx[:]))
-        for a in range(PASSES):
-            for b in range(BANKS):
-                col = (a * BANKS + b) * P
-                nc.tensor.matmul_mx(
-                    out=banks[b][:],
-                    lhsT=ws_c[:, 2 * col : 2 * col + 2 * P].bitcast(FP4X4),
-                    lhsT_scale=ws_s[:, col : col + P],
-                    rhs=v_c[a][:].bitcast(FP8X4),
-                    rhs_scale=v_s[:, a, :].bitcast(U8),
-                    start=(a == 0),
-                    stop=False,
-                )
+        ws_s.append(place([P, PASSES * K_PASS], U8, "ws_s1", at_v + 2 * KIB))
+        order_columns(ws_s[1], ws_sraw, 1, U8)
+
+        def add_short_term(g):
+            for a in range(PASSES):
+                for t in range(PACK):
+                    col = (a * PACK + t) * P
+                    nc.tensor.matmul_mx(
+                        out=banks[g * PACK + t][:],
+                        lhsT=ws_c[g][:, 2 * col : 2 * col + 2 * P].bitcast(FP4X4),
+                        lhsT_scale=ws_s[g][:, col : col + P],
+                        rhs=v_c[a][:].bitcast(FP8X4),
+                        rhs_scale=v_s[:, a, :].bitcast(U8),
+                        start=(a == 0),
+                        stop=False,
+                    )
+
+        add_short_term(0)
+
+        bd_col = place([P, P], F32, "bd_col", at_v + 4 * KIB)
+        bc_col = place([P, QUAD], F32, "bc_col", at_v + 5 * KIB)
+        nc.vector.transpose(bd_col[:], bd_planes[:])
+        nc.vector.transpose(bc_col[:], bc_rows[:])
 
         def wl_view(g, a, first, count):
             rows = wl_first[:, :, g * K_PASS : (g + 1) * K_PASS] if a == 0 else wl_second[g][:]
@@ -202,6 +216,7 @@ def tile_list_session_drift_novelty_kernel(
         )
         subtract_in_pairs(0, 0)
         subtract_in_pairs(0, 1)
+        add_short_term(1)
         subtract_long_term(1, 0, 0, PACK, neg_scalar)
         subtract_in_pairs(1, 1)
 
@@ -210,7 +225,8 @@ def tile_list_session_drift_novelty_kernel(
         h_s = [tile([P, S], U8, "h_s%d" % g) for g in range(PASSES)]
         for g in range(PASSES):
             for t in range(PACK):
-                nc.scalar.activation(h_rows[g][:, t, :], banks[g * PACK + t][:], ACT.Abs, bias=bd_col[:, g, t : t + 1])
+                at = QUAD * t + BD_STEP * g + BIAS_ROW
+                nc.scalar.activation(h_rows[g][:, t, :], banks[g * PACK + t][:], ACT.Abs, bias=bd_col[:, at : at + 1])
 
         def interleave(copy, packed, g, cols):
             copy(
@@ -275,5 +291,5 @@ def tile_list_session_drift_novelty_kernel(
                     stop=(a == order[1]),
                 )
             res = tile([P, S], F32, "res%d" % u)
-            nc.scalar.activation(res[:], banks[u][:], ACT.Sigmoid, bias=bc_col[:, u : u + 1])
+            nc.scalar.activation(res[:], banks[u][:], ACT.Sigmoid, bias=bc_col[:, BC_STEP * u + BIAS_ROW : BC_STEP * u + BIAS_ROW + 1])
             nc.sync.dma_start(out[u * P : (u + 1) * P, :], res[:])

from contextlib import ExitStack

import concourse.mybir as mybir

K, H, T, S, T2, S2 = 1024, 1024, 2048, 512, 4096, 1024
FLOPS = 2 * (2 * K * H * S + H * S2 * S)

F32 = mybir.dt.float32
BF16 = mybir.dt.bfloat16
I32 = mybir.dt.int32
U32 = mybir.dt.uint32
U16 = mybir.dt.uint16
U8 = mybir.dt.uint8
FP8X4 = mybir.dt.float8_e4m3fn_x4
FP4X4 = mybir.dt.float4_e2m1fn_x4
ACT = mybir.ActivationFunctionType
ALU = mybir.AluOpType

P = 128
PACK = 4
K_PASS = P * PACK
PASSES = 2
QUADS = 4
QUAD = P // QUADS
ROWS = 4
WORD = 4
BANKS = 8
KIB = 1024
V2_ROW = 4
TABLE_FIRST, TABLE_STEP = 32, 2
BC_STEP = QUAD // (S2 // P)
BD_STEP = QUAD // PASSES
BIAS_ROW = 1
GATHERS = (((0, 512), (512, 512)), ((0, 256), (256, 256), (512, 512)))
SCALE_RUNS = ((0, 256), (256, 768))
ALIGN = 256
QUAD_ORDER = (0, 2, 1, 3)
RUN = 4
WARM_UPS = 4


def tile_list_session_drift_novelty_kernel(
    tc, tab_words, tab_scales, offs, wl, ws_words, ws_scales, bd, tab2_words, tab2_scales, offs2, bc, out
):
    nc = tc.nc
    with ExitStack() as ctx:
        keep = ctx.enter_context(tc.tile_pool(name="keep", bufs=1))
        placed = ctx.enter_context(tc.tile_pool(name="placed", bufs=1))
        psum = ctx.enter_context(tc.psum_pool(name="psum", bufs=1))

        def tile(shape, dtype, name):
            return keep.tile(shape, dtype, name=name, align_bytes=ALIGN)

        def place(shape, dtype, name, offset):
            return placed.tile(shape, dtype, name=name, offset=offset, align_bytes=ALIGN)

        at_v2 = 0
        at_v = at_v2 + PASSES * WORD * T2
        at_pairs = at_v + PASSES * WORD * T
        at_late = at_pairs + 4 * KIB

        idx = keep.tile([P, S // 16], U16, name="idx")
        idx2 = keep.tile([P, S2 // 16], U16, name="idx2")
        banks = [psum.tile([P, S], F32, name="bank%d" % b) for b in range(BANKS)]
        ws_raw = tile([P, PASSES, 2 * H // WORD], I32, "ws_raw")
        ws_sraw = tile([P, PASSES, H // WORD], I32, "ws_sraw")
        ws_c = [tile([P, PASSES * K_PASS * 2], U8, "ws_c0")]
        ws_s = [tile([P, PASSES * K_PASS], U8, "ws_s0")]
        tab2_s = place([P, T2 // WORD], I32, "tab2_s", at_v2 + WORD * T2 - T2 // 2)
        zeros = place([P, P], F32, "zeros", at_v)
        bc_rows = tile([P, QUAD], F32, "bc_rows")
        bd_rows = tile([P, P], F32, "bd_rows")
        bd_planes = tile([P, P], F32, "bd_planes")
        v_s = tile([P, PASSES, S // WORD], I32, "v_s")
        v2_s = [tile([P, PASSES, count // WORD], I32, "v2_s%d" % first) for first, count in SCALE_RUNS]
        v_g = tile([P, S], U8, "v_g")
        v2_g = tile([P, S2], U8, "v2_g")

        def load_scale_table(dst, src):
            rows = slice(TABLE_FIRST, TABLE_FIRST + TABLE_STEP * PASSES * QUADS * ROWS, TABLE_STEP)
            nc.sync.dma_start(dst[rows, :], src.rearrange("a q c -> q a c").bitcast(I32))

        def move_scale_rows(dst, row, src, quad):
            span = TABLE_STEP * PASSES * ROWS
            first = TABLE_FIRST + span * quad
            nc.sync.dma_start(
                dst[QUAD * quad + row : QUAD * quad + row + ROWS, :, :],
                src[first : first + span : TABLE_STEP, :].bitcast(I32),
            )

        def order_columns(dst, src, g, dtype):
            columns = src[:].rearrange("p a c -> p (a c)").bitcast(dtype)
            nc.vector.tensor_copy(
                dst[:].bitcast(dtype).rearrange("p (a t m) -> p a t m", t=PACK, m=P),
                columns.rearrange("p (a g m t) -> p g a t m", g=PASSES, t=PACK, m=P)[:, g],
            )

        with tc.tile_pool(name="first", bufs=1) as first_pool:
            tab_s = first_pool.tile([P, T // WORD], I32, name="tab_s", align_bytes=ALIGN)
            nc.gpsimd.memset(ws_sraw[:], 0)
            nc.vector.memset(tab_s[:], 0)
            nc.vector.memset(tab2_s[:], 0)
            nc.vector.memset(zeros[:], 0.0)
            nc.vector.tensor_copy(bd_rows[:], zeros[:])
            nc.vector.memset(bc_rows[:], 0.0)
            nc.vector.memset(v_s[:], 0)
            for part in v2_s:
                nc.vector.memset(part[:], 0)
            nc.sync.dma_start(idx[:], offs)
            nc.sync.dma_start(idx2[:], offs2)
            nc.sync.dma_start(ws_raw[:], ws_words.rearrange("a p c -> p a c").bitcast(I32))
            load_scale_table(tab_s, tab_scales)
            for s in range(ROWS):
                nc.sync.dma_start(
                    ws_sraw[s:P:QUAD, :, :],
                    ws_scales[:, s : QUADS * ROWS : ROWS, :].rearrange("a q c -> q a c").bitcast(I32),
                )
            load_scale_table(tab2_s, tab2_scales)
            tab_w = place([P, PASSES, T], I32, "tab_w", at_v)
            nc.sync.dma_start(tab_w[:], tab_words.rearrange("a p t i -> p a (t i)").bitcast(I32))
            nc.sync.dma_start(bd_rows[BIAS_ROW:P:BD_STEP, :], bd.rearrange("(g h c) -> h g c", g=PASSES, h=QUADS))
            nc.sync.dma_start(bc_rows[BIAS_ROW:P:BC_STEP, :], bc.rearrange("(u h m) -> h u m", h=QUADS, m=QUAD))
            order_columns(ws_c[0], ws_raw, 0, U16)
            nc.vector.tensor_copy(v_g[:], tab_s[:].bitcast(U8).indirect(idx[:]))
        late = ctx.enter_context(tc.tile_pool(name="late", bufs=1))
        for quad in QUAD_ORDER:
            move_scale_rows(v_s, 0, v_g, quad)
        wl_rows = wl.rearrange("(a p j) c -> a p j c", a=PASSES, j=PACK)
        wl_first = late.tile([P, PACK, H], F32, name="wl_first", align_bytes=ALIGN)
        nc.sync.dma_start(wl_first[:], wl_rows[0])
        wl_second = []
        for g in range(PASSES):
            wl_second.append(late.tile([P, PACK, K_PASS], F32, name="wl_second%d" % g, tag="second%d" % g, align_bytes=ALIGN))
            nc.sync.dma_start(wl_second[g][:], wl_rows[1][:, :, g * K_PASS : (g + 1) * K_PASS])

        order_columns(ws_s[0], ws_sraw, 0, U8)
        ws_c.append(late.tile([P, PASSES * K_PASS * 2], U8, name="ws_c1", align_bytes=ALIGN))
        order_columns(ws_c[1], ws_raw, 1, U16)
        nc.vector.tensor_copy(v2_g[:], tab2_s[:].bitcast(U8).indirect(idx2[:]))
        tab2_w = [place([P, T2], I32, "tab2_w%d" % a, at_v2 + a * WORD * T2) for a in range(PASSES)]
        moves = [(part, first, count, quad) for part, (first, count) in zip(v2_s, SCALE_RUNS) for quad in QUAD_ORDER]
        for a in range(PASSES):
            nc.sync.dma_start(tab2_w[a][:], tab2_words[a].rearrange("p t i -> p (t i)").bitcast(I32))
            for part, first, count, quad in moves[0:1] if a == 0 else moves[1:]:
                move_scale_rows(part, V2_ROW, v2_g[:, first : first + count], quad)

        nc.scalar.activation(
            bd_planes[:].rearrange("p (t m) -> p t m", t=PACK), bd_rows[:].rearrange("p (m t) -> p t m", t=PACK), ACT.Copy
        )

        v_c = [tile([P, S], U32, "v_c%d" % a) for a in range(PASSES)]
        for a in range(PASSES):
            nc.vector.tensor_copy(v_c[a][:], tab_w[:, a, :].bitcast(U32).indirect(idx[:]))
        ws_s.append(place([P, PASSES * K_PASS], U8, "ws_s1", at_v + 2 * KIB))
        order_columns(ws_s[1], ws_sraw, 1, U8)

        def add_short_term(g):
            for a in range(PASSES):
                for t in range(PACK):
                    col = (a * PACK + t) * P
                    nc.tensor.matmul_mx(
                        out=banks[g * PACK + t][:],
                        lhsT=ws_c[g][:, 2 * col : 2 * col + 2 * P].bitcast(FP4X4),
                        lhsT_scale=ws_s[g][:, col : col + P],
                        rhs=v_c[a][:].bitcast(FP8X4),
                        rhs_scale=v_s[:, a, :].bitcast(U8),
                        start=(a == 0),
                        stop=False,
                    )

        add_short_term(0)

        bd_col = place([P, P], F32, "bd_col", at_v + 4 * KIB)
        bc_col = place([P, QUAD], F32, "bc_col", at_v + 5 * KIB)
        nc.vector.transpose(bd_col[:], bd_planes[:])
        nc.vector.transpose(bc_col[:], bc_rows[:])

        def wl_view(g, a, first, count):
            rows = wl_first[:, :, g * K_PASS : (g + 1) * K_PASS] if a == 0 else wl_second[g][:]
            return rows.rearrange("p j (m t) -> p m j t", t=PACK)[:, :, :, first : first + count]

        def subtract_long_term(g, a, first, count, neg):
            name = "%d%d%d" % (g, a, first)
            if count == PACK:
                codes = late.tile([P, count * P], U32, name="wl_c" + name, tag="second0", align_bytes=ALIGN)
            else:
                codes = tile([P, count * P], U32, "wl_c" + name)
            scales = tile([P, count * P], U8, "wl_s" + name)
            nc.vector.quantize_mx(
                out=codes[:].bitcast(FP8X4), scales=scales[:], in_=neg[:].rearrange("p t m j -> p (t m j)")
            )
            for t in range(count):
                nc.tensor.matmul_mx(
                    out=banks[g * PACK + first + t][:],
                    lhsT=codes[:, t * P : (t + 1) * P].bitcast(FP8X4),
                    lhsT_scale=scales[:, t * P : (t + 1) * P],
                    rhs=v_c[a][:].bitcast(FP8X4),
                    rhs_scale=v_s[:, a, :].bitcast(U8),
                    start=False,
                    stop=(a == PASSES - 1),
                )

        def subtract_in_pairs(g, a):
            negs = []
            for n in range(2):
                negs.append(place([P, 2, P, PACK], BF16, "neg%d%d%d" % (g, a, n), at_pairs + n * 2 * KIB))
                nc.vector.tensor_scalar(
                    negs[n][:].rearrange("p t m j -> p m j t"), wl_view(g, a, 2 * n, 2), -1.0, None, ALU.mult
                )
            for n in range(2):
                subtract_long_term(g, a, 2 * n, 2, negs[n])

        neg_scalar = tile([P, PACK, P, PACK], BF16, "neg10")
        nc.scalar.activation(
            neg_scalar[:].rearrange("p t m j -> p m j t"), wl_view(1, 0, 0, PACK), ACT.Copy, scale=-1.0
        )
        subtract_in_pairs(0, 0)
        subtract_in_pairs(0, 1)
        add_short_term(1)
        subtract_long_term(1, 0, 0, PACK, neg_scalar)
        subtract_in_pairs(1, 1)

        h_rows = [tile([P, PACK, S], BF16, "h_rows%d" % g) for g in range(PASSES)]
        h_c = [tile([P, S], U32, "h_c0")]
        h_s = [tile([P, S], U8, "h_s%d" % g) for g in range(PASSES)]
        for g in range(PASSES):
            for t in range(PACK):
                at = QUAD * t + BD_STEP * g + BIAS_ROW
                nc.scalar.activation(h_rows[g][:, t, :], banks[g * PACK + t][:], ACT.Abs, bias=bd_col[:, at : at + 1])

        def interleave(copy, packed, g, cols):
            copy(
                packed[:, cols, :].rearrange("p (c i) t -> p c t i", i=RUN),
                h_rows[g][:, :, cols].rearrange("p t (c i) -> p c t i", i=RUN),
            )

        def quantise_drift(packed, g, cols):
            nc.vector.quantize_mx(
                out=h_c[g][:, cols].bitcast(FP8X4),
                scales=h_s[g][:, cols],
                in_=packed[:, cols, :].rearrange("p n t -> p (n t)"),
            )

        halves = (slice(0, S // 2), slice(S // 2, S))

        def gather_v2(words, a):
            for first, count in GATHERS[a]:
                nc.vector.tensor_copy(
                    words[:, first : first + count],
                    tab2_w[a][:].bitcast(U32).indirect(idx2[:, first // 16 : (first + count) // 16]),
                )

        packed0 = place([P, S, PACK], BF16, "packed0", at_pairs)
        for cols in halves:
            interleave(nc.vector.tensor_copy, packed0, 0, cols)
        for cols in halves:
            quantise_drift(packed0, 0, cols)
        v2_first = place([P, S2], U32, "v2_first", at_pairs)
        gather_v2(v2_first, 0)
        h_c.append(place([P, S], U32, "h_c1", at_v2))
        packed1 = place([P, S, PACK], BF16, "packed1", at_late)
        for cols in halves:
            interleave(nc.scalar.copy, packed1, 1, cols)
        for cols in halves:
            quantise_drift(packed1, 1, cols)
        for rep in range(WARM_UPS):
            nc.tensor.matmul_mx(
                out=banks[0][:],
                lhsT=v2_first[:, 0:P].bitcast(FP8X4),
                lhsT_scale=h_s[0][:, 0:P],
                rhs=h_c[0][:].bitcast(FP8X4),
                rhs_scale=h_s[0][:],
                start=True,
                stop=True,
            )
        v2_c = [v2_first, place([P, S2], U32, "v2_last", at_late)]
        gather_v2(v2_c[1], 1)

        for u in range(S2 // P):
            run = max(c for c, (first, count) in enumerate(SCALE_RUNS) if first <= u * P)
            col = u * P - SCALE_RUNS[run][0]
            order = (0, 1) if u == 0 else (1, 0)
            for a in order:
                nc.tensor.matmul_mx(
                    out=banks[u][:],
                    lhsT=v2_c[a][:, u * P : (u + 1) * P].bitcast(FP8X4),
                    lhsT_scale=v2_s[run][V2_ROW:P, a, col // WORD : (col + P) // WORD].bitcast(U8),
                    rhs=h_c[a][:].bitcast(FP8X4),
                    rhs_scale=h_s[a][:],
                    start=(a == order[0]),
                    stop=(a == order[1]),
                )
            res = tile([P, S], F32, "res%d" % u)
            nc.scalar.activation(res[:], banks[u][:], ACT.Sigmoid, bias=bc_col[:, BC_STEP * u + BIAS_ROW : BC_STEP * u + BIAS_ROW + 1])
            nc.sync.dma_start(out[u * P : (u + 1) * P, :], res[:])
